import numpy as np, ml_dtypes
CORES = [40,64,80,88,96,104,120,144]
N = 8
import mx_ref
BF = ml_dtypes.bfloat16
def pick(q, e):
    c = np.concatenate([q[0].reshape(128, -1, 4), np.zeros((128, 1, 4), np.uint8)], axis=1); s = np.concatenate([q[1], np.ones((16, 1), np.uint8)], axis=1)
    return (np.ascontiguousarray(c[:, e].reshape(128, -1)), np.ascontiguousarray(s[:, e]))
def join(*qs):
    return (np.concatenate([q[0] for q in qs], axis=1), np.concatenate([q[1] for q in qs], axis=1))
def put(q, e, v):
    c, s = q[0].reshape(128, -1, 4).copy(), q[1].copy(); c[:, e] = v[0].reshape(128, -1, 4); s[:, e] = v[1]
    return (c.reshape(128, -1), s)
def pk(c, s):
    return (np.ascontiguousarray(c), mx_ref.live(s))
def emit(q):
    return q[0], q[1]
def decode(q):
    o = []
    for b in range(4):
        e = np.zeros((128, 128, 4), np.float32); e[np.arange(128), np.arange(128), b] = 1
        o.append(mx_ref.matmul(mx_ref.quantize(e.reshape(128, 512).astype(BF)), q))
    return np.stack(o, axis=2).reshape(128, -1)
def f(rng, *shape):
    return mx_ref.flush((rng.standard_normal(shape, dtype=np.float32) * np.exp2(rng.integers(-2, 3, shape[:-1] + (1,)))).astype(BF))
def wide(rng, *shape, cols=0):
    v = rng.standard_normal(shape, dtype=np.float32) * np.exp2(rng.integers(-12, 13, shape)).astype(np.float32)
    if cols: v *= np.repeat(np.exp2(rng.integers(-cols, cols + 1, shape[:-2] + (1, shape[-1] // 4))) * (rng.random(shape[:-2] + (1, shape[-1] // 4)) > 0.0625), 4, axis=-1).astype(np.float32)
    return mx_ref.flush(v.astype(BF))
P, B, K, KO = 384, 48, 16, 16
def big(v):
    v = v.astype(np.float32)
    v[np.abs(v) < np.float32(2.0 ** -16)] = 0
    return v.astype(BF)
def toward(rng, u, size):
    sg = np.where(u[0, :, :4].astype(np.float32) < 0, -1.0, 1.0)
    s = np.asarray(size)[..., None, :, None]
    v = (1 + rng.random(s.shape[:-3] + (128, s.shape[-2], 4))) * sg[:, None, :] * s
    return v.reshape(v.shape[:-2] + (-1,)).astype(np.float32)
def near(rng, size):
    s = np.abs(np.asarray(size))[..., None, :, None]
    v = (rng.random(s.shape[:-3] + (128, s.shape[-2], 4)) - 0.5) * 0.25 * s
    return v.reshape(v.shape[:-2] + (-1,)).astype(np.float32)
def plain(rng):
    u = np.array(f(rng, 128, 512))
    u[:, 4:] = 0
    return {"gr": big(f(rng, N, 128, 4 * P)), "er": big(f(rng, N, 128, 4 * P).astype(np.float32) * np.float32(0.125)), "fo": big(f(rng, N, 128, 4 * B)), "u": np.stack([u] * N), "w": f(rng, N, 128, 512)}
def setup_inputs(rng):
    return plain(rng)
def setup_inputs_same(rng):
    d = plain(rng)
    size, own = np.full((B, N), 2.0 ** -5), np.full((N, B), 2.0 ** -4)
    for o in range(N):
        m = rng.permutation(B)
        size[m[:K], o] = np.exp2(rng.integers(0, 3, K))
        own[o, m[K:K + KO // 2]] = 2.0 ** 8
    size = size * rng.choice([-1.0, 1.0], size.shape)
    size = np.tile(size.reshape(P), (N, 1))
    own = own * rng.choice([-1.0, 1.0], own.shape)
    return {**d, "gr": big(toward(rng, d["u"], size)), "er": big(near(rng, size)), "fo": big(toward(rng, d["u"], own))}
def setup_inputs_apart(rng):
    d = plain(rng)
    size = np.full((N, B, N), 2.0 ** -5)
    for o in range(N):
        m, a = rng.permutation(B), rng.permutation(N)
        for s in range(N): size[s, m[(a[s] * K + np.arange(K)) % B], o] = np.exp2(rng.integers(0, 3, K))
    size = (size * rng.choice([-1.0, 1.0], size.shape)).reshape(N, P)
    e, fo = big(near(rng, size)), np.array(d["fo"])
    a = rng.permutation(N)
    e[a[0]] = 0
    fo[a[1]] = 0
    return {**d, "gr": big(toward(rng, d["u"], size)), "er": e, "fo": fo}
def setup_inputs_cancel(rng):
    d = plain(rng)
    size, own = np.full((B, N), 2.0 ** 5), np.full((N, B), 2.0 ** -13)
    gone = np.zeros(N, int)
    for o in range(N):
        m = rng.permutation(B)[:K]
        size[m, o] = np.exp2(rng.integers(11, 13, K))
        own[o, m] = np.exp2(rng.integers(-10, -8, K))
        own[o, m[:K // 2]] = 0
        gone[o] = m[K - 1]
    h = int(rng.integers(0, N))
    own[h] = 0
    size = np.tile(size.reshape(P), (N, 1)) * rng.choice([-1.0, 1.0], (N, P))
    g, e, fo = big(toward(rng, d["u"], size)), big(near(rng, size)), big(toward(rng, d["u"], own))
    a = rng.permutation(N)
    g[a[1::2]] = -g[a[::2]]
    e[a[1::2]] = -e[a[::2]]
    gv, ev, fv = g.reshape(N, 128, B, N, 4), e.reshape(N, 128, B, N, 4), fo.reshape(N, 128, B, 4)
    half = np.where(d["u"][0, :, :4].astype(np.float32) < 0, -1.0, 1.0) * 2.0 ** 11
    part = np.ones(N)
    part[a[1::2]] = -1
    part[a[:2]] = -1
    for o in range(N):
        if o == h: continue
        m, x = int(gone[o]), half * rng.choice([-1.0, 1.0])
        gv[:, :, m, o] = (part[:, None, None] * x).astype(BF)
        ev[:, :, m, o] = 0
        fv[o, :, m] = (2 * x).astype(BF)
    return {**d, "gr": g, "er": e, "fo": fo}
def setup_inputs_ties(rng):
    d = plain(rng)
    u = np.zeros((128, 512), BF)
    u[:, :4] = ((1 + rng.random((128, 4))) * 2.0 ** 29 * rng.choice([-1.0, 1.0], (128, 4))).astype(BF)
    d["u"] = np.stack([u] * N)
    size, own, tied = np.zeros((B, N)), np.ones((N, B)), np.zeros((N, B), bool)
    for o in range(N):
        t = int(rng.integers(2, min(K, KO)))
        m = rng.permutation(B)
        size[m[:t], o] = 2.0 ** 23
        size[int(m[:t].min()), o] = 7 * 2.0 ** 20
        own[o, m[:t]] = 2.0 ** 23
        tied[o, np.sort(m[t:])[K - t:]] = True
    size = np.tile(size.reshape(P), (N, 1))
    hot = np.repeat(size > 0, 4, axis=1)[:, None, :]
    sg = np.repeat(rng.choice([-1.0, 1.0], (N, P)), 4, axis=1)[:, None, :]
    g = np.where(hot, toward(rng, d["u"], size), np.tile(toward(rng, d["u"], np.ones((N, 1))), (1, 1, P)) * sg)
    e = np.where(hot, near(rng, size), np.tile(near(rng, np.ones((N, 1))), (1, 1, P)) * sg)
    so = np.repeat(rng.choice([-1.0, 1.0], (N, B)), 4, axis=1)[:, None, :]
    fo = np.where(np.repeat(tied, 4, axis=1)[:, None, :], np.tile(toward(rng, d["u"], np.full((N, 1), 2.0 ** 9)), (1, 1, B)) * so, toward(rng, d["u"], own))
    return {**d, "gr": big(g), "er": big(e), "fo": big(fo)}
def setup_inputs_spread(rng):
    g, e, fo = big(wide(rng, N, 128, 4 * P, cols=8)), big(wide(rng, N, 128, 4 * P, cols=8)), big(wide(rng, N, 128, 4 * B, cols=8))
    gv, ev, fv = g.reshape(N, 128, B, N, 4), e.reshape(N, 128, B, N, 4), fo.reshape(N, 128, B, 4)
    top = np.array([225.0, 241.0, 255.0])[np.arange(128) // 8 % 3][:, None]
    r = int(rng.integers(0, N))
    for o in range(N):
        z = np.sort(rng.permutation(B)[int(rng.integers(0, K)):])
        for v in (gv, ev):
            v[r][:, z, o] = 0
            v[:, :, int(z[0]), o] = 0
        fv[o, :, int(z[0])] = (top * np.exp2(rng.integers(-14, -10, (128, 4))) * rng.choice([-1.0, 1.0], (128, 4))).astype(BF)
    return {**plain(rng), "gr": g, "er": e, "fo": fo}
def check_inputs(d):
    b = []
    for k, lo, hi in (("gr", -16, 24), ("er", -16, 24), ("fo", -16, 24), ("u", -30, 30), ("w", -30, 30)):
        v = np.abs(d[k].astype(np.float32))
        if not (np.isfinite(v).all() and ((v == 0) | (v >= 2.0 ** lo) & (v <= 2.0 ** hi)).all()): b.append("a value of " + k)
    u = d["u"].astype(np.float32)
    if (u[:, :, 4:] != 0).any(): b.append("u has numbers behind its column 0")
    if (u != u[:1]).any(): b.append("u isn't the same on all ranks")
    return b
def best(z, k):
    return np.argsort(-np.abs(z), kind="stable")[:k]
def reference(gr, er, fo, u, w):
    oc, osc = np.zeros((N, 128, 4 * (P + B)), np.uint8), np.zeros((N, 16, P + B), np.uint8)
    nb, y = np.zeros((N, 1, N * KO), np.float32), np.zeros((N, 128, N * KO), np.float32)
    qu = [mx_ref.quantize(u[r]) for r in range(N)]
    sent, held, werr = [], [], []
    for s in range(N):
        v = (gr[s].astype(np.float32) + decode(mx_ref.quantize(er[s]))).astype(BF)
        q = mx_ref.quantize(v)
        z = mx_ref.matmul(qu[s], q)[0]
        e = [best(z[o::N], K) for o in range(N)]
        n = np.concatenate([N * e[o] + o for o in range(N)])
        dq = decode(q)
        left = mx_ref.quantize((v.astype(np.float32) - dq).astype(BF))
        werr.append(put(q, n, pick(left, n)))
        sent.append(e)
        held.append(dq.reshape(128, P, 4))
    win, numbers = [], []
    for o in range(N):
        qf = mx_ref.quantize(fo[o])
        a, named = decode(qf).reshape(128, B, 4).copy(), np.zeros(B, bool)
        for s in range(N):
            m = sent[s][o]
            a[:, m] = a[:, m] + held[s][:, N * m + o]
            named[m] = True
        a = a.reshape(128, 4 * B).astype(BF)
        m = np.flatnonzero(named)
        p = put(qf, m, pick(mx_ref.quantize(a), m))
        t = best(mx_ref.matmul(qu[o], p)[0], KO)
        left = mx_ref.quantize((a.astype(np.float32) - decode(p)).astype(BF))
        oc[o], osc[o] = emit(join(werr[o], put(p, t, pick(left, t))))
        win.append(pick(p, t))
        numbers.append(N * t + o)
    every = join(*win)
    for r in range(N):
        nb[r, 0] = np.concatenate(numbers)
        y[r] = mx_ref.matmul(mx_ref.quantize(w[r]), every)
    return {"oc": oc, "osc": osc, "nb": nb, "y": y}

@@ -1,0 +1,611 @@
+from concourse.bass import DstId, RemoteDMATransfer
+from concourse.mybir import dt, AluOpType, AxisListType, ActivationFunctionType
+
+P, B, K = 384, 48, 16
+SEG = K + 1
+LW = 144
+ZC = 8 * SEG
+TINY = 2.0 ** -120
+L0, Q0, E0 = 128, 256, 640
+PW = 128
+CW, SL, CS3, CWN, CSE, CS2, CALL = 512, 652, 908, 1292, 1420, 1548, 1676
+WN, Z0 = 96, 104
+X4, U8 = "float8_e4m3fn_x4", "uint8"
+
+SCRATCH = {"ps": ("psum", [128, 4096], "float32")}
+
+
+def _buf(name, n, d):
+    SCRATCH[name] = ("sbuf", [128, n], d)
+
+
+for _n, _w in (("qe", 384), ("ce", CALL), ("cu", 128), ("qq", 1024), ("sc", 192), ("hc", 48), ("hd", 18), ("land", LW), ("pq", 384), ("fx", 384),
+               ("pa", 128), ("pb", 256), ("cbt", 128), ("wb", 144), ("land2", 136), ("eo", 432), ("c2", 128), ("qw", 128)):
+    _buf(_n, _w, X4)
+    _buf(_n + "s", _w, U8)
+for _n, _w in (("et", 1536), ("gt", 1536), ("h", 1536), ("lf", 1536), ("ut", 8), ("ft", 192), ("wt", 512), ("ones", 520), ("ident", 520),
+               ("zt", 616), ("ur", 512), ("hh", 528), ("jrowe", 512), ("ow1", 512), ("stt", 1024), ("slt", 1024), ("fxt", 1536),
+               ("bb", 144), ("d0", 144), ("dx", 384), ("st", 1536), ("ste", 512), ("st2", 512), ("x2", 512), ("at", 512), ("oht", 512),
+               ("l2t", 512), ("lt", 512), ("so", 1536), ("bt", 48)):
+    _buf(_n, _w, "bfloat16")
+for _n, _w in (("ff", 32), ("kc", 4), ("r3", 4), ("r6", 8), ("r3b", 4), ("own", 48), ("ow2", 48), ("ow3", 48), ("row144", 144), ("row48", 48),
+               ("mkrow", 72), ("row16k", 24), ("thr", 144), ("thr2", 48), ("mk", 72), ("zs", 384), ("zg", 144), ("cum", 144),
+               ("zt2", 96), ("tt", 144), ("t3", 4), ("t4", 4), ("s3", 4), ("tin", 32), ("tto", 32), ("pf", 4), ("pg", 4),
+               ("junk", 8), ("sm", 4), ("m2", 4), ("m3", 4), ("mc", 4), ("zca", 4), ("rk", 4), ("tq", 48), ("tq2", 48), ("zab", 48), ("te", 4),
+               ("ysb", 128), ("nbt", 32), ("nbx", 32)):
+    _buf(_n, _w, "float32")
+for _n, _w in (("pidx", 4), ("ii", 12)):
+    _buf(_n, _w, "int32")
+for _n, _w in (("goff", 10), ("off1", 12), ("off3", 24), ("off4", 24), ("plist", 4), ("wl", 2), ("elist", 4)):
+    _buf(_n, _w, "uint16")
+
+SEMAPHORES = ["cv", "ct", "ca", "cg", "ls", "arr1", "arr2", "h1", "h2"] + ["d%d" % _k for _k in range(48)]
+
+
+def roles(core, T, topo):
+    direct = [d for d in T.cores if topo.same_plane(core, d)]
+    cross = [d for d in T.cores if d != core and d not in direct]
+    own = sorted(direct + [core])
+    hs = [c for c in topo.cores_of(core) if c not in T.cores and all([topo.may_write(c, d) for d in cross])]
+    near = [c for c in hs if topo.die(c) == topo.die(core)][:2]
+    far = [c for c in hs if topo.die(c) != topo.die(core)][:2]
+    ranks = [T.rank_of(c) for c in sorted(cross)] + [T.rank_of(c) for c in own]
+    units = [(ranks[2 * t], ranks[2 * t + 1]) for t in range(4)]
+    return direct, units, near, far
+
+
+def bits(es):
+    m = 0
+    for e in es:
+        m |= 1 << e
+    return m
+
+
+def split(engines, j, flip):
+    q = len(engines) // 4
+    cut = [0, q, 2 * q, 4 * q] if flip else [0, 2 * q, 3 * q, 4 * q]
+    return engines[cut[j]:cut[j + 1]]
+
+
+def tracker(g, T):
+    eng = {"v": g.vector, "t": g.tensor, "a": g.scalar, "g": g, "s": g.sync}
+    names = {"v": "cv", "t": "ct", "a": "ca", "g": "cg"}
+    cnt, known, waited, hist, nd = {}, {q: {} for q in eng}, {}, {}, [0]
+
+    def clash(a, b):
+        if a[2] <= b[1] or b[2] <= a[1]:
+            return False
+        return not (len(a) > 3 and len(b) > 3 and a[3] == b[3] and a[4] != b[4])
+
+    def wait(q, toks):
+        toks = [t for t in toks if known[q].get(t[0], 0) < t[1]]
+        best = {}
+        for t in toks:
+            if t[0] not in best or best[t[0]][1] < t[1]:
+                best[t[0]] = t
+        for t in list(best.values()):
+            if any([u is not t and u[2].get(t[0], 0) >= t[1] for u in best.values()]):
+                continue
+            eng[q].wait_ge(T.sem[t[0]], t[1])
+            waited[t[0]] = max(waited.get(t[0], 0), t[1])
+            for s, c in t[2].items():
+                known[q][s] = max(known[q].get(s, 0), c)
+
+    def hazards(q, reads, writes):
+        toks = []
+        for r in reads:
+            for (x, w, tok, e) in hist.get(r[0], []):
+                if r[0] == "ps":
+                    if e != q and clash(r, x): toks.append(tok)
+                elif w and clash(r, x): toks.append(tok)
+        for r in writes:
+            for (x, w, tok, e) in hist.get(r[0], []):
+                if r[0] == "ps":
+                    if e != q and clash(r, x): toks.append(tok)
+                elif clash(r, x): toks.append(tok)
+        return toks
+
+    def note(q, reads, writes, tok):
+        for r in reads: hist.setdefault(r[0], []).append((r, False, tok, q))
+        for r in writes: hist.setdefault(r[0], []).append((r, True, tok, q))
+
+    def op(q, fn, reads, writes):
+        wait(q, hazards(q, reads, writes))
+        s = names[q]
+        cnt[s] = cnt.get(s, 0) + 1
+        fn().then_inc(T.sem[s], 1)
+        ck = dict(known[q])
+        ck[s] = cnt[s]
+        note(q, reads, writes, (s, cnt[s], ck))
+
+    def dma(q, out, in_, reads, writes):
+        wait(q, hazards("dma", reads, writes))
+        s = "d%d" % nd[0]
+        nd[0] += 1
+        eng[q].dma_start(out, in_).then_inc(T.sem[s], 16)
+        cnt[s] = 16
+        ck = dict(known[q])
+        ck[s] = 16
+        note("dma", reads, writes, (s, 16, ck))
+
+    def before(q, reads):
+        wait(q, hazards("dma", reads, []))
+
+    def arrive(s, total, writes):
+        cnt[s] = total
+        note("far", [], writes, (s, total, {s: total}))
+
+    def finish(extra):
+        for s, c in extra.items(): cnt[s] = c
+        for s in cnt:
+            if waited.get(s, 0) < cnt[s]: g.wait_ge(T.sem[s], cnt[s])
+
+    return op, dma, before, arrive, finish
+
+
+def helper(g, core, T, topo):
+    home = [c for c in T.cores if core in topo.cores_of(c)]
+    if not home:
+        return
+    src = home[0]
+    s = T.rank_of(src)
+    direct, units, near, far = roles(src, T, topo)
+    if core in far:
+        t, codes = far.index(core), True
+    elif core in near:
+        t, codes = near.index(core), False
+    else:
+        return
+    a, b = [T.cores[r] for r in units[t]]
+
+    def did(d):
+        rid, pid = topo.addr(d, core)
+        return DstId(rid=rid, pnc=pid)
+
+    def view(n, lo, hi):
+        return T[n][:, lo:hi].bitcast(dt.uint8) if codes else T[n + "s"][:, lo:hi]
+    es = topo.engines(core, a)
+    half = len(es) // 2
+    g.wait_ge(T.sem.h1, half)
+    g.remote_dma_fused([
+        RemoteDMATransfer(dst_ids=[did(a)], dma_engine_mask=bits(es[:half]), remote_sem=T.sem.arr1, srcs=[view("hc", 0, SEG)], dsts=[view("land", SEG * s, SEG * s + SEG)]),
+        RemoteDMATransfer(dst_ids=[did(b)], dma_engine_mask=bits(es[half:]), remote_sem=T.sem.arr1, srcs=[view("hc", 48 - SEG, 48)], dsts=[view("land", SEG * s, SEG * s + SEG)]),
+    ], local_sem=T.sem.ls)
+    g.wait_ge(T.sem.h2, len(es))
+    g.remote_dma_fused([RemoteDMATransfer(dst_ids=[did(a), did(b)], dma_engine_mask=bits(es), remote_sem=T.sem.arr2, srcs=[view("hd", 0, SEG)],
+                                          dsts=[view("land2", SEG * s, SEG * s + SEG)] * 2)], local_sem=T.sem.ls)
+    g.wait_ge(T.sem.ls, 2 * len(es))
+
+
+def rank_program(g, core, T, topo):
+    rank = T.rank_of(core)
+    if rank is None:
+        return helper(g, core, T, topo)
+    direct, units, near, far = roles(core, T, topo)
+    op, dma, before, arrive, finish = tracker(g, T)
+    A, F = AluOpType, ActivationFunctionType
+    v, ten, sca = g.vector, g.tensor, g.scalar
+    ps = T.ps
+
+    def fill(n, lo, hi, val, step=1):
+        op("v", lambda: v.memset(T[n][:, lo:hi:step], val), [], [(n, lo, hi)])
+
+    def iota(n, w, pattern, base=0, cm=0):
+        op("g", lambda: g.iota(T[n][:, 0:w], pattern, base, cm, allow_small_or_imprecise_dtypes=True), [], [(n, 0, w)])
+
+    def select(n, lo, hi, src, w, pattern, cmp, base, cm):
+        op("g", lambda: g.affine_select(T[n][:, lo:hi], T[src][:, 0:w], pattern, cmp, 0.0, base, cm), [(src, 0, w)], [(n, lo, hi)])
+
+    def ts(out, o, in0, i, s1, s2, op0, op1=None, more=()):
+        rd = [i] + list(more)
+        if op1 is None:
+            op("v", lambda: v.tensor_scalar(out, in0, s1, None, op0), rd, [o])
+        else:
+            op("v", lambda: v.tensor_scalar(out, in0, s1, s2, op0, op1), rd, [o])
+
+    def tt(out, o, in0, i0, in1, i1, opx, more=()):
+        op("v", lambda: v.tensor_tensor(out, in0, in1, opx), [i0, i1] + list(more), [o])
+
+    def copy(out, o, in_, i):
+        op("v", lambda: v.tensor_copy(out, in_), [i], [o])
+
+    def act(out, o, in_, i, func, more=(), **kw):
+        op("a", lambda: sca.activation(out, in_, func, **kw), [i] + list(more), o if isinstance(o, list) else [o])
+
+    def quant(n, c, w, tile, a):
+        op("v", lambda: v.quantize_mx(T[n][:, c:c + w], T[n + "s"][:, c:c + w], T[tile][:, a:a + 4 * w]),
+           [(tile, a, a + 4 * w)], [(n, c, c + w), (n + "s", c, c + w)])
+
+    def mm(bank, w, ln, l0, rn, r0, start=True, stop=True):
+        op("t", lambda: ten.matmul_mx(ps[:, 512 * bank:512 * bank + w], T[ln][:, l0:l0 + 128], T[ln + "s"][:, l0:l0 + 128],
+                                      T[rn][:, r0:r0 + w], T[rn + "s"][:, r0:r0 + w], start, stop),
+           [(ln, l0, l0 + 128), (ln + "s", l0, l0 + 128), (rn, r0, r0 + w), (rn + "s", r0, r0 + w)], [("ps", bank, bank + 1)])
+
+    def pick(on, o0, sn, w0, w1, ln, e0, e1):
+        w = 16 * (e1 - e0)
+        op("v", lambda: v.tensor_copy(T[on][:, o0:o0 + w].bitcast(dt.uint32), T[sn][:, w0:w1].bitcast(dt.uint32).indirect(T[ln][:, e0:e1])),
+           [(sn, w0, w1), (ln, e0, e1)], [(on, o0, o0 + w)])
+        op("a", lambda: sca.activation(T[on + "s"][:, o0:o0 + w], T[sn + "s"][:, w0:w1].indirect(T[ln][:, e0:e1]), F.Copy),
+           [(sn + "s", w0, w1), (ln, e0, e1)], [(on + "s", o0, o0 + w)])
+
+    def bank(k, lo, hi, step=1):
+        return ps[:, 512 * k + lo:512 * k + hi:step]
+
+    def copymx(q, dn, d0, sn, s0, w):
+        dma(q, T[dn][:, d0:d0 + w].bitcast(dt.uint8), T[sn][:, s0:s0 + w].bitcast(dt.uint8), [(sn, s0, s0 + w)], [(dn, d0, d0 + w)])
+        dma(q, T[dn + "s"][:, d0:d0 + w], T[sn + "s"][:, s0:s0 + w], [(sn + "s", s0, s0 + w)], [(dn + "s", d0, d0 + w)])
+
+    def zeros(n, lo, hi):
+        dma("s", T[n][:, lo:hi], T.zt[:, Z0:Z0 + hi - lo], [("zt", Z0, Z0 + hi - lo)], [(n, lo, hi)])
+
+    def load(q, dst, src, k):
+        sl = slice(4 * PW * k, 4 * PW * k + 4 * PW)
+        dma(q, T[dst][:, sl], T[src][:, sl], [], [(dst, 4 * PW * k, 4 * PW * k + 4 * PW)])
+    load("s", "et", "er", 0)
+    dma("a", T.ut[:, 0:4], T.u[:, 0:4], [], [("ut", 0, 8)])
+    load("a", "gt", "gr", 0)
+    load("s", "et", "er", 1)
+    load("a", "gt", "gr", 1)
+    load("s", "et", "er", 2)
+    load("a", "gt", "gr", 2)
+    dma("s", T.ft[:, 0:192], T.fo[:, 0:192], [], [("ft", 0, 192)])
+    dma("s", T.wt[:, 0:512], T.w[:, 0:512], [], [("wt", 0, 512)])
+
+    op("g", lambda: g.iota(T.pidx[:, 0:1], [[0, 1]], 0, 1), [], [("pidx", 0, 4)])
+    fill("ones", 0, 520, 1.0)
+    select("ident", 0, 516, "ones", 516, [[-1, 516]], A.is_equal, 3, 4)
+    iota("r3", 3, [[128, 3]])
+    iota("r6", 6, [[128, 3], [1, 2]])
+    iota("jrowe", 512, [[0, 8], [1, 16], [64, 4]])
+    iota("row144", 144, [[-16, 3], [1, 48]])
+    jrow = T.jrowe[:, 0:512:4]
+
+    def ibit(k, s1, s2, op0, op1=None):
+        ts(T.ii[:, k:k + 1], ("ii", k, k + 1), T.pidx[:, 0:1], ("pidx", 0, 4), s1, s2, op0, op1)
+
+    def col(k):
+        return T.ff[:, k:k + 1]
+
+    def fc(k, src, s1, s2, op0, op1, more=()):
+        ts(col(k), ("ff", k, k + 1), col(src), ("ff", src, src + 1), s1, s2, op0, op1, [("ff", m, m + 1) for m in more])
+    ibit(0, 15, None, A.bitwise_and)
+    ibit(1, 4, None, A.logical_shift_right)
+    ibit(2, 4, 14, A.logical_shift_right, A.bitwise_and)
+    ibit(3, 1, None, A.bitwise_and)
+    ibit(4, 15, 1, A.bitwise_and, A.logical_shift_right)
+    copy(T.ii[:, 5:6], ("ii", 5, 6), T.pidx[:, 0:1], ("pidx", 0, 4))
+    ibit(6, 7, None, A.bitwise_and)
+    copy(T.ff[:, 0:7], ("ff", 0, 7), T.ii[:, 0:7], ("ii", 0, 7))
+    fc(9, 1, float(rank), None, A.is_equal, None)
+    fill("zt", 0, 616, 0.0)
+    fc(16, 0, 8.0, col(1), A.mult, A.add, [1])
+    fc(17, 0, 8.0, col(2), A.mult, A.add, [2])
+    ts(T.ii[:, 8:9], ("ii", 8, 9), col(16), ("ff", 16, 17), 16.0, None, A.add)
+    ts(T.ii[:, 9:10], ("ii", 9, 10), T.ii[:, 8:9], ("ii", 8, 9), 480, None, A.bitwise_and)
+    copy(col(21), ("ff", 21, 22), T.ii[:, 9:10], ("ii", 9, 10))
+    fc(20, 16, col(21), None, A.subtract, None, [21])
+    fill("hh", 512, 528, 0.0)
+    op("v", lambda: v.memset(T.hh[:, 3:512:4], 0.0), [], [("hh", 0, 512, 4, 3)])
+    for b in range(4):
+        quant("ce", 128 * b, 128, "ident", 3 - b)
+
+    act(T.own[:, 0:48], ("own", 0, 48), T.ones[:, 0:48], ("ones", 0, 48), F.Copy, scale=99.0)
+    for t in range(4):
+        for k, o in ((3 * t, units[t][0]), (3 * t + 2, units[t][1])):
+            act(T.own[:, 4 * k:4 * k + 4], ("own", 4 * k, 4 * k + 4), T.ones[:, 0:4], ("ones", 0, 4), F.Copy, scale=float(o))
+    act(T.kc[:, 0:1], ("kc", 0, 1), T.ones[:, 0:1], ("ones", 0, 1), F.Copy, scale=-15.5)
+    act(T.kc[:, 1:2], ("kc", 1, 2), T.ones[:, 0:1], ("ones", 0, 1), F.Copy, scale=-1800.0)
+    act(T.ow2[:, 0:48], ("ow2", 0, 48), T.own[:, 0:48], ("own", 0, 48), F.Abs, [("ff", 1, 2)], bias=col(1), scale=-1.0)
+    act(T.ow3[:, 0:48], ("ow3", 0, 48), T.ow2[:, 0:48], ("ow2", 0, 48), F.Relu, [("ones", 0, 1)], bias=T.ones[:, 0:1], scale=-1.0)
+    act(T.ow1[:, 0:512], ("ow1", 0, 512), T.ones[:, 0:512], ("ones", 0, 512), F.Copy, [("ff", 9, 10)], scale=col(9))
+    act(T.kc[:, 2:3], ("kc", 2, 3), col(0), ("ff", 0, 1), F.Copy, scale=TINY)
+    act(T.kc[:, 3:4], ("kc", 3, 4), col(5), ("ff", 5, 6), F.Copy, scale=TINY)
+    for e in range(4):
+        act(T.ur[:, e:512:4], ("ur", 0, 512, 4, e), T.zt[:, Z0:Z0 + 128], ("zt", Z0, Z0 + 128), F.Identity, [("ut", 0, 8)], bias=T.ut[:, e:e + 1])
+    act(T.thr[:, 0:144], ("thr", 0, 144), T.row144[:, 0:144], ("row144", 0, 144), F.Relu, [("kc", 2, 3)], bias=T.kc[:, 2:3], scale=-TINY)
+    for h in range(2):
+        select("slt", 512 * h, 512 * h + 512, "ow1", 512, [[0, 4], [-2, 32], [16, 4]], A.is_equal, -16 * rank - h, 1)
+    select("st", 1024, 1536, "ones", 512, [[0, 8], [-1, 16], [-256, 4]], A.is_equal, 512 - 16 * rank, 1)
+
+    BE = ((0, 1, 2, 3), (4, 5, 6, 7), (0, 1, 2, 4))
+    BS = (3, 5, 6)
+
+    def errors(k):
+        quant("qe", PW * k, PW, "et", 4 * PW * k)
+        for b in range(4):
+            mm(BE[k][b], PW, "ce", 128 * b, "qe", PW * k)
+
+    def values(k, b):
+        lo, hi = 4 * PW * k, 4 * PW * k + 4 * PW
+        sl = slice(lo + b, hi, 4)
+        n = BE[k][b]
+        tt(T.h[:, sl], ("h", lo, hi, 4, b), bank(n, 0, PW), ("ps", n, n + 1), T.gt[:, sl], ("gt", lo, hi), A.add)
+
+    def codes_of(k):
+        quant("qq", Q0 + PW * k, PW, "h", 4 * PW * k)
+
+    def scores(k):
+        n = BS[k]
+        mm(n, PW, "cu", 0, "qq", Q0 + PW * k)
+        act(T.zs[:, PW * k:PW * k + PW], ("zs", PW * k, PW * k + PW), bank(n, 0, PW), ("ps", n, n + 1), F.Abs)
+    errors(0)
+    ts(T.ff[:, 22:25], ("ff", 22, 25), T.r3[:, 0:3], ("r3", 0, 3), col(21), 128.0, A.add, A.add, [("ff", 21, 22)])
+    ts(T.goff[:, 0:3], ("goff", 0, 3), T.r3[:, 0:3], ("r3", 0, 3), col(16), None, A.add, None, [("ff", 16, 17)])
+    ts(T.goff[:, 3:9], ("goff", 3, 9), T.r6[:, 0:6], ("r6", 0, 6), col(17), None, A.add, None, [("ff", 17, 18)])
+    for c in range(3):
+        act(T.zt[:, c:48:4], ("zt", 0, 48, 4, c), T.ow3[:, c:48:4], ("ow3", 0, 48), F.Copy, [("ff", 22 + c, 23 + c)], scale=col(22 + c))
+    act(T.zt[:, 48:96], ("zt", 48, 96), T.ow3[:, 0:48], ("ow3", 0, 48), F.Copy, [("ff", 20, 21)], scale=col(20))
+
+    def pattern(c, bias, rd):
+        o = 512 * c
+        act(T.stt[:, o:o + 512], ("stt", o, o + 512), T.jrowe[:, 0:512], ("jrowe", 0, 512), F.Abs, rd, bias=bias, scale=-1.0)
+        act(T.st[:, o:o + 512], ("st", o, o + 512), T.stt[:, o:o + 512], ("stt", o, o + 512), F.Relu, [("ff", 9, 10)], bias=col(9), scale=-1.0)
+    pattern(0, col(0), [("ff", 0, 1)])
+    quant("cu", 0, 128, "ur", 0)
+    values(0, 0)
+    values(0, 1)
+    errors(1)
+    values(0, 2)
+    values(0, 3)
+    codes_of(0)
+    values(1, 0)
+    values(1, 1)
+    errors(2)
+    values(1, 2)
+    values(1, 3)
+    codes_of(1)
+    scores(0)
+    scores(1)
+    for b in range(4):
+        values(2, b)
+    codes_of(2)
+    scores(2)
+    for b in range(2):
+        mm(b, 384, "ce", 128 * b, "qq", Q0)
+    before("s", [("et", 1024, 1536)])
+    for k in range(3):
+        zeros("fxt", 512 * k, 512 * k + 512)
+    zeros("oht", 0, 512)
+    zeros("l2t", 0, 512)
+    zeros("at", 384, 512)
+    zeros("x2", 0, 512)
+    zeros("lt", 192, 512)
+    copymx("s", "pb", B, "ce", 0, 128 - B)
+    fill("d0", 0, 144, 1.0)
+    fill("d0", 0, 144, 0.0, 48)
+    quant("ce", CW, 140, "zt", 0)
+    fc(11, 0, 64.0, None, A.add, None)
+    second = [u for u in units if rank in u][0][1] == rank
+    lp, dlt = (0, 1) if second else (K, 0)
+    fc(18, 6, float(SEG), float(dlt), A.mult, A.add)
+
+    op("v", lambda: v.tensor_copy(T.zg[:, 0:144], T.zs[:, 0:384].indirect(T.goff[:, 0:9])), [("zs", 0, 384), ("goff", 0, 9)], [("zg", 0, 144)])
+    op("v", lambda: v.transpose(T.zt2[:, 0:96], T.zg[:, 48:144]), [("zg", 48, 144)], [("zt2", 0, 96)])
+    for c in range(3):
+        ts(T.tt[:, 48 * c:48 * c + 48], ("tt", 48 * c, 48 * c + 48), T.zg[:, 0:48], ("zg", 0, 48), T.zt2[:, 32 * c:32 * c + 1], -1.0, A.subtract, A.mult, [("zt2", 0, 96)])
+    tt(T.bb[:, 0:144], ("bb", 0, 144), T.tt[:, 0:144], ("tt", 0, 144), T.thr[:, 0:144], ("thr", 0, 144), A.is_lt)
+    op("v", lambda: v.tensor_tensor_scan(T.cum[:, 0:144], T.d0[:, 0:144], T.bb[:, 0:144], 0.0, A.mult, A.add), [("d0", 0, 144), ("bb", 0, 144)], [("cum", 0, 144)])
+    act(T.t3[:, 0:3], ("t3", 0, 3), T.cum[:, 47:144:48], ("cum", 0, 144), F.Sign, [("kc", 0, 1)], bias=T.kc[:, 0:1])
+    act(T.t4[:, 0:3], ("t4", 0, 3), T.t3[:, 0:3], ("t3", 0, 3), F.Copy, scale=240.0)
+    for c in range(3):
+        ts(T.hh[:, c:512:4], ("hh", 0, 512, 4, c), jrow, ("jrowe", 0, 512), T.cum[:, 48 * c + 47:48 * c + 48], None, A.is_equal, None, [("cum", 0, 144)])
+    tt(T.hh[:, 512:515], ("hh", 512, 515), T.t4[:, 0:3], ("t4", 0, 3), T.cum[:, 47:144:48], ("cum", 0, 144), A.max)
+    quant("qq", 0, 132, "hh", 0)
+    for k in range(2):
+        mm(2, 128, "qq", 0, "ce", CW + 12 * k, k == 0, k == 1)
+    mm(7, 384, "ce", 256, "qq", Q0)
+    mm(3, 384, "ce", 384, "qq", Q0)
+
+    def left_over(b, n):
+        sl = slice(b, 1536, 4)
+        tt(T.lf[:, sl], ("lf", 0, 1536, 4, b), T.h[:, sl], ("h", 0, 1536), bank(n, 0, 384), ("ps", n, n + 1), A.subtract)
+    left_over(0, 0)
+    ts(T.off1[:, 0:12], ("off1", 0, 12), bank(2, 0, 12), ("ps", 2, 3), float(L0), None, A.add)
+    pick("sc", 0, "qq", 0, 640, "off1", 0, 6)
+    pick("sc", 96, "qq", 0, 640, "off1", 6, 12)
+
+    def did(d):
+        rid, pid = topo.addr(d, core)
+        return DstId(rid=rid, pnc=pid)
+
+    def mxv(n, lo, hi, codes):
+        return T[n][:, lo:hi].bitcast(dt.uint8) if codes else T[n + "s"][:, lo:hi]
+    off = topo.engines(core, direct[0])
+    hop = [e for e in topo.engines(core, far[0]) if e not in off]
+    half = len(hop) // 2
+    run = {}
+    for t in range(4):
+        run[units[t][0]] = (48 * t, 48 * t + SEG)
+        run[units[t][1]] = (48 * t + 48 - SEG, 48 * t + 48)
+    me = (SEG * rank, SEG * rank + SEG)
+    left = [0]
+    for codes, hs in ((True, far), (False, near)):
+        nm = "sc" if codes else "scs"
+        before("g", [(nm, 0, 96)])
+        g.remote_dma_fused([RemoteDMATransfer(dst_ids=[did(hs[t])], dma_engine_mask=bits(hop[half * t:half * t + half]), remote_sem=T.sem.h1,
+                                              srcs=[mxv("sc", 48 * t, 48 * t + 48, codes)], dsts=[mxv("hc", 0, 48, codes)]) for t in range(2)], local_sem=T.sem.ls)
+        left[0] += 2 * half
+    for codes in (True, False):
+        nm = "sc" if codes else "scs"
+        before("g", [(nm, 96, 192)])
+        tr = []
+        for j in range(3):
+            r = T.rank_of(direct[j])
+            es = split(off, j, not codes)
+            tr.append(RemoteDMATransfer(dst_ids=[did(direct[j])], dma_engine_mask=bits(es), remote_sem=T.sem.arr1,
+                                        srcs=[mxv("sc", run[r][0], run[r][1], codes)], dsts=[mxv("land", me[0], me[1], codes)]))
+            left[0] += len(es)
+        g.remote_dma_fused(tr, local_sem=T.sem.ls)
+    copymx("s", "land", me[0], "sc", run[rank][0], SEG)
+    copymx("s", "land", ZC, "qq", 130, 2)
+    iota("r3b", 3, [[16, 3]])
+    iota("row48", 48, [[1, 48]])
+    select("dx", 0, 384, "ones", 384, [[0, 48], [1, 8]], A.not_equal, 0, 0)
+    iota("mkrow", 72, [[-8, 3], [1, 24]])
+    iota("row16k", 24, [[16, 24]])
+
+    for e in range(4):
+        act(T.fxt[:, e:1536:32], ("fxt", 0, 1536, 32, e), T.ft[:, e:192:4], ("ft", 0, 192), F.Copy)
+    pattern(1, col(11), [("ff", 11, 12)])
+    left_over(1, 1)
+    quant("fx", 0, 384, "fxt", 0)
+    quant("ce", SL, 256, "slt", 0)
+    BD = (4, 5, 6)
+    for b in range(3):
+        mm(BD[b], 384, "ce", 128 * b, "fx", 0, True, False)
+    left_over(2, 7)
+    left_over(3, 3)
+    for k, n in ((0, 7), (1, 3)):
+        mm(n, 192, "ce", 384, "fx", 192 * k, True, False)
+    quant("qq", E0, 384, "lf", 0)
+    ts(T.mc[:, 0:3], ("mc", 0, 3), T.r3b[:, 0:3], ("r3b", 0, 3), col(0), None, A.add, None, [("ff", 0, 1)])
+    ts(T.m2[:, 0:3], ("m2", 0, 3), T.mc[:, 0:3], ("mc", 0, 3), 2.0, 0.5, A.mult, A.add)
+    quant("ce", CS3, 384, "st", 0)
+    fc(25, 1, 2.5, 16.0, A.is_lt, A.mult)
+    fc(26, 1, 2.5, None, A.is_lt, None)
+    fill("l2t", 2, 3, float(rank))
+    for e in range(4):
+        act(T.at[:, 4 + e:384:8], ("at", 0, 384, 8, 4 + e), T.ft[:, e:192:4], ("ft", 0, 192), F.Copy)
+    act(T.zt[:, WN:WN + 1], ("zt", WN, WN + 1), col(1), ("ff", 1, 2), F.Copy, [("ff", 25, 26)], scale=col(25))
+    act(T.zt[:, WN + 4:WN + 5], ("zt", WN + 4, WN + 5), col(0), ("ff", 0, 1), F.Copy, [("ff", 26, 27)], scale=col(26))
+    act(T.thr2[:, 0:48], ("thr2", 0, 48), T.row48[:, 0:48], ("row48", 0, 48), F.Relu, [("kc", 3, 4)], bias=T.kc[:, 3:4], scale=-TINY)
+
+    total = 0
+    for s in range(8):
+        if s == rank: continue
+        src = T.cores[s]
+        sd = roles(src, T, topo)[0]
+        if core in sd:
+            es = topo.engines(src, core)
+            j = sd.index(core)
+            total += len(split(es, j, False)) + len(split(es, j, True))
+        else:
+            total += len(off)
+    arrive("arr1", total, [(n, SEG * s, SEG * s + SEG) for s in range(8) if s != rank for n in ("land", "lands")])
+    for h in range(2):
+        mm(h, 8 * SEG, "ce", SL + 128 * h, "land", 0)
+    for k in range(2):
+        copy(T.tin[:, 16 * k:16 * k + 8], ("tin", 16 * k, 16 * k + 8), bank(0, lp, ZC, SEG), ("ps", 0, 1))
+        act(T.tin[:, 16 * k + 8:16 * k + 16], ("tin", 16 * k + 8, 16 * k + 16), bank(1, lp, ZC, SEG), ("ps", 1, 2), F.Copy)
+    op("v", lambda: v.transpose(T.tto[:, 0:32], T.tin[:, 0:32]), [("tin", 0, 32)], [("tto", 0, 32)])
+    ts(T.off4[:, 0:24], ("off4", 0, 24), T.tto[:, 0:24], ("tto", 0, 32), col(18), float(ZC), A.add, A.min, [("ff", 18, 19)])
+    for k in range(2):
+        pick("pq", 192 * k, "land", 0, LW, "off4", 12 * k, 12 * k + 12)
+    for c in range(3):
+        mm((2, 0, 1)[c], 8 * SEG, "ce", CS3 + 128 * c, "land", 0)
+    mm(7, 192, "ce", 384, "pq", 0, False, True)
+    for b in range(3):
+        mm(BD[b], 384, "ce", 128 * b, "pq", 0, False, True)
+    mm(3, 192, "ce", 384, "pq", 192, False, True)
+    for c in range(3):
+        k = (2, 0, 1)[c]
+        act(T.junk[:, 0:8], [("junk", 0, 8), ("sm", c, c + 1)], bank(k, lp, ZC, SEG), ("ps", k, k + 1), F.Copy, accum_out=T.sm[:, c:c + 1])
+    act(T.pf[:, 0:3], ("pf", 0, 3), T.sm[:, 0:3], ("sm", 0, 3), F.Sign, [("kc", 1, 2)], bias=T.kc[:, 1:2])
+    for c in range(3):
+        act(T.pg[:, c:c + 1], ("pg", c, c + 1), T.pf[:, c:c + 1], ("pf", 0, 3), F.Identity, [("m2", 0, 3)], bias=T.m2[:, c:c + 1], scale=0.5)
+
+    def sums(b, lo, hi, n):
+        o = 384 * b
+        op("v", lambda: v.tensor_tensor_scan(T.so[:, o + lo:o + hi], T.dx[:, 0:hi - lo], bank(n, 0, hi - lo), 0.0, A.mult, A.add),
+           [("dx", 0, 384), ("ps", n, n + 1)], [("so", o + lo, o + hi)])
+
+    def summed(q, b, lo, hi):
+        o = 384 * b
+        out, in_ = T.at[:, lo + b:hi:8], T.so[:, o + lo + 7:o + hi:8]
+        if q == "a":
+            act(out, ("at", lo, hi, 8, b), in_, ("so", o + lo, o + hi), F.Copy)
+        else:
+            copy(out, ("at", lo, hi, 8, b), in_, ("so", o + lo, o + hi))
+    sums(3, 0, 192, 7)
+    summed("a", 3, 0, 192)
+    quant("ce", CWN, 128, "zt", WN)
+    fc(27, 1, 128.0, None, A.mult, None)
+    ts(T.m3[:, 0:3], ("m3", 0, 3), T.r3[:, 0:3], ("r3", 0, 3), col(27), 15.5, A.is_equal, A.mult, [("ff", 27, 28)])
+    fc(19, 3, 8.0, col(1), A.mult, A.add, [1])
+    sums(0, 0, 384, 4)
+    summed("a", 0, 0, 384)
+    sums(1, 0, 384, 5)
+    summed("a", 1, 0, 384)
+    copy(T.plist[:, 0:3], ("plist", 0, 3), T.pg[:, 0:3], ("pg", 0, 3))
+    sums(2, 0, 384, 6)
+    summed("a", 2, 0, 384)
+    sums(3, 192, 384, 3)
+    summed("v", 3, 192, 384)
+    quant("pa", 0, 128, "at", 0)
+    pick("pb", 0, "pa", 0, 128, "plist", 0, 3)
+
+    mm(1, 128, "cu", 0, "pb", 0)
+    mm(0, 128, "pb", 0, "cu", 0)
+    act(T.zab[:, 0:48], ("zab", 0, 48), bank(1, 0, 48), ("ps", 1, 2), F.Abs)
+    for e in range(3):
+        ts(T.ste[:, e:512:4], ("ste", 0, 512, 4, e), jrow, ("jrowe", 0, 512), col(19), None, A.is_equal, None, [("ff", 19, 20)])
+    ts(T.ste[:, 3:512:4], ("ste", 0, 512, 4, 3), jrow, ("jrowe", 0, 512), col(0), None, A.is_equal, None, [("ff", 0, 1)])
+    op("v", lambda: v.tensor_reduce(T.zca[:, 0:1], bank(0, 0, 1), AxisListType.X, A.max, apply_absolute_value=True), [("ps", 0, 1)], [("zca", 0, 1)])
+    ts(T.tq[:, 0:48], ("tq", 0, 48), T.zab[:, 0:48], ("zab", 0, 48), T.zca[:, 0:1], -1.0, A.subtract, A.mult, [("zca", 0, 1)])
+    tt(T.bt[:, 0:48], ("bt", 0, 48), T.tq[:, 0:48], ("tq", 0, 48), T.thr2[:, 0:48], ("thr2", 0, 48), A.is_lt)
+    op("v", lambda: v.tensor_reduce(T.rk[:, 0:1], T.bt[:, 0:48], AxisListType.X, A.add), [("bt", 0, 48)], [("rk", 0, 1)])
+    ts(T.oht[:, 0:512:4], ("oht", 0, 512, 4, 0), jrow, ("jrowe", 0, 512), T.rk[:, 0:1], None, A.is_equal, None, [("rk", 0, 1)])
+    quant("cbt", 0, 128, "oht", 0)
+    mm(2, 128, "cbt", 0, "ce", CWN)
+    quant("ce", CSE, 128, "ste", 0)
+    ts(T.wl[:, 0:1], ("wl", 0, 1), bank(2, 0, 1), ("ps", 2, 3), bank(2, 1, 2), None, A.add, None)
+    copy(T.l2t[:, 0:2], ("l2t", 0, 2), bank(2, 0, 2), ("ps", 2, 3))
+    pick("wb", 0, "pb", 0, 128, "wl", 0, 1)
+    quant("wb", 16, 128, "l2t", 0)
+
+    for codes, hs in ((True, far), (False, near)):
+        nm = "wb" if codes else "wbs"
+        before("g", [(nm, 0, SEG)])
+        src, dst = mxv("wb", 0, SEG, codes), mxv("land2", me[0], me[1], codes)
+        g.remote_dma_fused([
+            RemoteDMATransfer(dst_ids=[did(x) for x in hs], dma_engine_mask=bits(hop), remote_sem=T.sem.h2, srcs=[src], dsts=[mxv("hd", 0, SEG, codes)] * 2),
+            RemoteDMATransfer(dst_ids=[did(x) for x in direct], dma_engine_mask=bits(off), remote_sem=T.sem.arr2, srcs=[src], dsts=[dst] * 3),
+        ], local_sem=T.sem.ls)
+        left[0] += len(hop) + len(off)
+    copymx("s", "land2", me[0], "wb", 0, SEG)
+
+    ts(T.s3[:, 0:3], ("s3", 0, 3), T.cum[:, 47:144:48], ("cum", 0, 144), 15.5, None, A.is_lt)
+    ts(T.mk[:, 0:72], ("mk", 0, 72), T.mkrow[:, 0:72], ("mkrow", 0, 72), col(4), None, A.is_equal, None, [("ff", 4, 5)])
+    for c in range(3):
+        ts(T.x2[:, c:96:4], ("x2", 0, 96, 4, c), T.mk[:, 24 * c:24 * c + 24], ("mk", 0, 72), T.s3[:, c:c + 1], None, A.mult, None, [("s3", 0, 3)])
+    ts(T.x2[:, 131:143:4], ("x2", 128, 144), T.m3[:, 0:3], ("m3", 0, 3), T.rk[:, 0:1], 128.0, A.is_gt, A.mult, [("rk", 0, 1)])
+    quant("c2", 0, 128, "x2", 0)
+    mm(3, 128, "ce", CSE, "c2", 0)
+    for b in range(4):
+        mm(4 + b, 128, "ce", 128 * b, "pb", 0)
+    for e in range(4):
+        act(T.st2[:, e:512:4], ("st2", 0, 512, 4, e), T.ident[:, 3:515:4], ("ident", 0, 516), F.Copy, scale=(8.0, 8.0, 1.0, 0.0)[e])
+    quant("qw", 0, 128, "wt", 0)
+    ts(T.tq2[:, 0:24], ("tq2", 0, 24), bank(3, 0, 24), ("ps", 3, 4), 384.0, col(0), A.mult, A.add, [("ff", 0, 1)])
+    tt(T.te[:, 0:3], ("te", 0, 3), bank(3, 32, 35), ("ps", 3, 4), T.mc[:, 0:3], ("mc", 0, 3), A.add)
+    tt(T.tq[:, 0:24], ("tq", 0, 24), T.tq2[:, 0:24], ("tq2", 0, 24), T.row16k[:, 0:24], ("row16k", 0, 24), A.add)
+    copy(T.off3[:, 0:24], ("off3", 0, 24), T.tq[:, 0:24], ("tq", 0, 24))
+    pick("eo", 0, "qq", Q0, 1024, "off3", 0, 24)
+    dma("s", T.oc[:, 0:1536], T.eo[:, 0:384].bitcast(dt.uint8), [("eo", 0, 384)], [("oc", 0, 1)])
+    for k in range(4):
+        dma("s", T.osc[4 * k:4 * k + 4, 0:384], T.eos[32 * k:32 * k + 4, 0:384], [("eos", 0, 384)], [("osc", k, k + 1)])
+    copy(T.elist[:, 0:3], ("elist", 0, 3), T.te[:, 0:3], ("te", 0, 3))
+    for b in range(4):
+        tt(T.lt[:, b:192:4], ("lt", 0, 192, 4, b), T.at[:, b:384:8], ("at", 0, 384), bank(4 + b, 0, 48), ("ps", 4 + b, 5 + b), A.subtract)
+    quant("pb", 128, 128, "lt", 0)
+    pick("eo", 384, "pb", 0, 256, "elist", 0, 3)
+    dma("s", T.oc[:, 1536:1728], T.eo[:, 384:432].bitcast(dt.uint8), [("eo", 384, 432)], [("oc", 1, 2)])
+    for k in range(4):
+        dma("s", T.osc[4 * k:4 * k + 4, 384:432], T.eos[32 * k:32 * k + 4, 384:432], [("eos", 384, 432)], [("osc", 4 + k, 5 + k)])
+    quant("ce", CS2, 128, "st2", 0)
+    fill("nbt", 0, 32, 0.0)
+
+    arrive("arr2", 7 * 2 * len(off), [(n, SEG * s, SEG * s + SEG) for s in range(8) if s != rank for n in ("land2", "land2s")])
+    mm(1, 136, "qw", 0, "land2", 0)
+    mm(0, 136, "qw", 0, "land2", 0)
+    mm(3, 136, "ce", CS2, "land2", 0)
+    for q in range(3, 8):
+        act(T.ysb[:, 16 * q:16 * q + 16], ("ysb", 16 * q, 16 * q + 16), bank(1, SEG * q, SEG * q + 16), ("ps", 1, 2), F.Copy)
+    for q in range(3):
+        copy(T.ysb[:, 16 * q:16 * q + 16], ("ysb", 16 * q, 16 * q + 16), bank(0, SEG * q, SEG * q + 16), ("ps", 0, 1))
+    copy(T.nbt[:, 0:8], ("nbt", 0, 8), bank(3, K, 136, SEG), ("ps", 3, 4))
+    op("v", lambda: v.transpose(T.nbx[:, 0:32], T.nbt[:, 0:32]), [("nbt", 0, 32)], [("nbx", 0, 32)])
+    dma("s", T.y[:, 0:48], T.ysb[:, 0:48], [("ysb", 0, 48)], [("y", 0, 48)])
+    dma("s", T.nb[0:1, 0:128], T.nbx[0:8, 0:16], [("nbx", 0, 32)], [("nb", 0, 1)])
+    dma("a", T.y[:, 48:128], T.ysb[:, 48:128], [("ysb", 48, 128)], [("y", 48, 128)])
+    finish({"ls": left[0]})

@@ -6,10 +6,12 @@ SEG = K + 1
 LW = 144
 ZC = 8 * SEG
 TINY = 2.0 ** -120
-L0, Q0, E0 = 128, 256, 640
+H0, L0, Q0, E0 = 16, 144, 256, 640
+S0 = 96
 PW = 128
-CW, SL, CS3, CWN, CSE, CS2, CALL = 512, 652, 908, 1292, 1420, 1548, 1676
-WN, Z0 = 96, 104
+CW, SL, CS3, CS2, CX, CALL = 512, 652, 908, 1292, 1420, 1574
+WN, WX, WE, WZ, WALL = 24, 26, 50, 54, 178
+SW = B + P
 X4, U8 = "float8_e4m3fn_x4", "uint8"
 
 SCRATCH = {"ps": ("psum", [128, 4096], "float32")}
@@ -19,33 +21,33 @@ def _buf(name, n, d):
     SCRATCH[name] = ("sbuf", [128, n], d)
 
 
-for _n, _w in (("qe", 384), ("ce", CALL), ("cu", 128), ("qq", 1024), ("sc", 192), ("hc", 48), ("hd", 18), ("land", LW), ("pq", 384), ("fx", 384),
-               ("pa", 128), ("pb", 256), ("cbt", 128), ("wb", 144), ("land2", 136), ("eo", 432), ("c2", 128), ("qw", 128)):
+for _n, _w in (("qe", 384), ("ce", CALL), ("cu", 128), ("qq", 1024), ("sc", 288), ("hc", 192), ("hd", 68), ("land", LW), ("pq", 384), ("fx", 384),
+               ("pb", 256), ("cbt", 128), ("wb", 144), ("land2", 136), ("eo", 432), ("c2", 128), ("c3", 128), ("qw", 128)):
     _buf(_n, _w, X4)
     _buf(_n + "s", _w, U8)
-for _n, _w in (("et", 1536), ("gt", 1536), ("h", 1536), ("lf", 1536), ("ut", 8), ("ft", 192), ("wt", 512), ("ones", 520), ("ident", 520),
-               ("zt", 616), ("ur", 512), ("hh", 528), ("jrowe", 512), ("ow1", 512), ("stt", 1024), ("slt", 1024), ("fxt", 1536),
-               ("bb", 144), ("d0", 144), ("dx", 384), ("st", 1536), ("ste", 512), ("st2", 512), ("x2", 512), ("at", 512), ("oht", 512),
-               ("l2t", 512), ("lt", 512), ("so", 1536), ("bt", 48)):
+for _n, _w in (("et", 1536), ("gt", 1536), ("h", 1536), ("lf", 1536), ("ut", 8), ("ft", 192), ("wt", 512), ("ident", 520), ("pj", 128), ("jr", 128),
+               ("zt", 768), ("ur", 512), ("hh", 528), ("ow1", 512), ("slt", 1024), ("fxt", 1536), ("st3", 520), ("sta", 128),
+               ("bb", 144), ("d0", 144), ("cum", 144), ("dx", 384), ("st2", 512), ("al", 704), ("oht", 512), ("so", 4 * SW), ("bt", 48)):
     _buf(_n, _w, "bfloat16")
-for _n, _w in (("ff", 32), ("kc", 4), ("r3", 4), ("r6", 8), ("r3b", 4), ("own", 48), ("ow2", 48), ("ow3", 48), ("row144", 144), ("row48", 48),
-               ("mkrow", 72), ("row16k", 24), ("thr", 144), ("thr2", 48), ("mk", 72), ("zs", 384), ("zg", 144), ("cum", 144),
-               ("zt2", 96), ("tt", 144), ("t3", 4), ("t4", 4), ("s3", 4), ("tin", 32), ("tto", 32), ("pf", 4), ("pg", 4),
-               ("junk", 8), ("sm", 4), ("m2", 4), ("m3", 4), ("mc", 4), ("zca", 4), ("rk", 4), ("tq", 48), ("tq2", 48), ("zab", 48), ("te", 4),
-               ("ysb", 128), ("nbt", 32), ("nbx", 32)):
+for _n, _w in (("ff", 40), ("own", 48), ("ow2", 48), ("ow3", 48), ("row", 144), ("nk", 24), ("xa", 48), ("xb", 4), ("thr", 144), ("thr2", 48),
+               ("zs", 384), ("zg", 96), ("zt2", 64), ("tt", 144), ("t3", 4), ("t4", 4), ("s3", 4), ("tin", 32), ("tto", 32), ("pf", 4), ("pg", 4),
+               ("junk", 24), ("sm", 4), ("sa", 4), ("ba", 4), ("zca", 4), ("rk", 4), ("win", 4), ("tq", 48), ("tq2", 24), ("zab", 48), ("te", 4),
+               ("ysb", 128), ("pre", 8), ("nbt", 32), ("nbx", 32)):
     _buf(_n, _w, "float32")
 for _n, _w in (("pidx", 4), ("ii", 12)):
     _buf(_n, _w, "int32")
-for _n, _w in (("goff", 10), ("off1", 12), ("off3", 24), ("off4", 24), ("plist", 4), ("wl", 2), ("elist", 4)):
+for _n, _w in (("goff", 6), ("off1", 12), ("off3", 24), ("off4", 24), ("plist", 4), ("wl", 2), ("elist", 4)):
     _buf(_n, _w, "uint16")
 
-SEMAPHORES = ["cv", "ct", "ca", "cg", "ls", "arr1", "arr2", "h1", "h2"] + ["d%d" % _k for _k in range(48)]
+SEMAPHORES = ["cv", "ct", "ca", "cg", "ls1", "ls2", "arr1", "arr2", "h1", "h2"] + ["d%d" % _k for _k in range(40)]
 
 
 def roles(core, T, topo):
-    direct = [d for d in T.cores if topo.same_plane(core, d)]
-    cross = [d for d in T.cores if d != core and d not in direct]
-    own = sorted(direct + [core])
+    same = [d for d in T.cores if topo.same_plane(core, d)]
+    cross = [d for d in T.cores if d != core and d not in same]
+    own = sorted(same + [core])
+    x = own.index(core)
+    direct = own[x + 1:] + own[:x]
     hs = [c for c in topo.cores_of(core) if c not in T.cores and all([topo.may_write(c, d) for d in cross])]
     near = [c for c in hs if topo.die(c) == topo.die(core)][:2]
     far = [c for c in hs if topo.die(c) != topo.die(core)][:2]
@@ -67,15 +69,23 @@ def split(engines, j, flip):
     return engines[cut[j]:cut[j + 1]]
 
 
+def winners_at(r):
+    return (127, 76) if r % 2 == 0 else (0, 0)
+
+
 def tracker(g, T):
     eng = {"v": g.vector, "t": g.tensor, "a": g.scalar, "g": g, "s": g.sync}
     names = {"v": "cv", "t": "ct", "a": "ca", "g": "cg"}
     cnt, known, waited, hist, nd = {}, {q: {} for q in eng}, {}, {}, [0]
 
     def clash(a, b):
+        if a[0] == "ps":
+            return a[1] // 512 == b[1] // 512
         if a[2] <= b[1] or b[2] <= a[1]:
             return False
-        return not (len(a) > 3 and len(b) > 3 and a[3] == b[3] and a[4] != b[4])
+        if len(a) > 3 and len(b) > 3:
+            return not set(range(*a[1:4])).isdisjoint(range(*b[1:4]))
+        return True
 
     def wait(q, toks):
         toks = [t for t in toks if known[q].get(t[0], 0) < t[1]]
@@ -93,16 +103,10 @@ def tracker(g, T):
 
     def hazards(q, reads, writes):
         toks = []
-        for r in reads:
-            for (x, w, tok, e) in hist.get(r[0], []):
-                if r[0] == "ps":
-                    if e != q and clash(r, x): toks.append(tok)
-                elif w and clash(r, x): toks.append(tok)
-        for r in writes:
-            for (x, w, tok, e) in hist.get(r[0], []):
-                if r[0] == "ps":
-                    if e != q and clash(r, x): toks.append(tok)
-                elif clash(r, x): toks.append(tok)
+        for rs, any_ in ((reads, False), (writes, True)):
+            for r in rs:
+                for (x, w, tok, e) in hist.get(r[0], []):
+                    if (e != q if r[0] == "ps" else w or any_) and clash(r, x): toks.append(tok)
         return toks
 
     def note(q, reads, writes, tok):
@@ -114,9 +118,7 @@ def tracker(g, T):
         s = names[q]
         cnt[s] = cnt.get(s, 0) + 1
         fn().then_inc(T.sem[s], 1)
-        ck = dict(known[q])
-        ck[s] = cnt[s]
-        note(q, reads, writes, (s, cnt[s], ck))
+        note(q, reads, writes, (s, cnt[s], dict(known[q], **{s: cnt[s]})))
 
     def dma(q, out, in_, reads, writes):
         wait(q, hazards("dma", reads, writes))
@@ -124,9 +126,7 @@ def tracker(g, T):
         nd[0] += 1
         eng[q].dma_start(out, in_).then_inc(T.sem[s], 16)
         cnt[s] = 16
-        ck = dict(known[q])
-        ck[s] = 16
-        note("dma", reads, writes, (s, 16, ck))
+        note("dma", reads, writes, (s, 16, dict(known[q], **{s: 16})))
 
     def before(q, reads):
         wait(q, hazards("dma", reads, []))
@@ -135,10 +135,11 @@ def tracker(g, T):
         cnt[s] = total
         note("far", [], writes, (s, total, {s: total}))
 
-    def finish(extra):
-        for s, c in extra.items(): cnt[s] = c
+    def finish(q, only=None):
         for s in cnt:
-            if waited.get(s, 0) < cnt[s]: g.wait_ge(T.sem[s], cnt[s])
+            if waited.get(s, 0) < cnt[s] and (only is None or s[0] in only):
+                eng[q].wait_ge(T.sem[s], cnt[s])
+                waited[s] = cnt[s]
 
     return op, dma, before, arrive, finish
 
@@ -162,19 +163,23 @@ def helper(g, core, T, topo):
         rid, pid = topo.addr(d, core)
         return DstId(rid=rid, pnc=pid)
 
-    def view(n, lo, hi):
-        return T[n][:, lo:hi].bitcast(dt.uint8) if codes else T[n + "s"][:, lo:hi]
+    def view(n, lo):
+        return T[n][:, lo:lo + SEG].bitcast(dt.uint8) if codes else T[n + "s"][:, lo:lo + SEG]
     es = topo.engines(core, a)
     half = len(es) // 2
+    o = 0 if codes else S0 + B * t
     g.wait_ge(T.sem.h1, half)
     g.remote_dma_fused([
-        RemoteDMATransfer(dst_ids=[did(a)], dma_engine_mask=bits(es[:half]), remote_sem=T.sem.arr1, srcs=[view("hc", 0, SEG)], dsts=[view("land", SEG * s, SEG * s + SEG)]),
-        RemoteDMATransfer(dst_ids=[did(b)], dma_engine_mask=bits(es[half:]), remote_sem=T.sem.arr1, srcs=[view("hc", 48 - SEG, 48)], dsts=[view("land", SEG * s, SEG * s + SEG)]),
-    ], local_sem=T.sem.ls)
+        RemoteDMATransfer(dst_ids=[did(a)], dma_engine_mask=bits(es[:half]), remote_sem=T.sem.arr1, srcs=[view("hc", o)], dsts=[view("land", SEG * s)]),
+        RemoteDMATransfer(dst_ids=[did(b)], dma_engine_mask=bits(es[half:]), remote_sem=T.sem.arr1, srcs=[view("hc", o + B - SEG)], dsts=[view("land", SEG * s)]),
+    ], local_sem=T.sem.ls1)
+    to = [a, b] + (direct[2:] if t == 0 else [])
+    at, window = winners_at(s)
+    g.wait_ge(T.sem.ls1, len(es))
     g.wait_ge(T.sem.h2, len(es))
-    g.remote_dma_fused([RemoteDMATransfer(dst_ids=[did(a), did(b)], dma_engine_mask=bits(es), remote_sem=T.sem.arr2, srcs=[view("hd", 0, SEG)],
-                                          dsts=[view("land2", SEG * s, SEG * s + SEG)] * 2)], local_sem=T.sem.ls)
-    g.wait_ge(T.sem.ls, 2 * len(es))
+    g.remote_dma_fused([RemoteDMATransfer(dst_ids=[did(x) for x in to], dma_engine_mask=bits(es), remote_sem=T.sem.arr2, srcs=[view("hd", 0 if codes else at - window)],
+                                          dsts=[view("land2", SEG * s)] * len(to))], local_sem=T.sem.ls2)
+    g.wait_ge(T.sem.ls2, len(es))
 
 
 def rank_program(g, core, T, topo):
@@ -185,41 +190,76 @@ def rank_program(g, core, T, topo):
     op, dma, before, arrive, finish = tracker(g, T)
     A, F = AluOpType, ActivationFunctionType
     v, ten, sca = g.vector, g.tensor, g.scalar
-    ps = T.ps
 
-    def fill(n, lo, hi, val, step=1):
-        op("v", lambda: v.memset(T[n][:, lo:hi:step], val), [], [(n, lo, hi)])
+    def ap(x):
+        if not isinstance(x, tuple):
+            return x
+        return T[x[0]][:, x[1]:x[2]:x[3]] if len(x) > 3 else T[x[0]][:, x[1]:x[2]]
 
-    def iota(n, w, pattern, base=0, cm=0):
-        op("g", lambda: g.iota(T[n][:, 0:w], pattern, base, cm, allow_small_or_imprecise_dtypes=True), [], [(n, 0, w)])
+    def held(*xs):
+        return [x for x in xs if isinstance(x, tuple)]
 
-    def select(n, lo, hi, src, w, pattern, cmp, base, cm):
-        op("g", lambda: g.affine_select(T[n][:, lo:hi], T[src][:, 0:w], pattern, cmp, 0.0, base, cm), [(src, 0, w)], [(n, lo, hi)])
+    def bank(k, lo, hi, step=1):
+        return ("ps", 512 * k + lo, 512 * k + hi, step)
 
-    def ts(out, o, in0, i, s1, s2, op0, op1=None, more=()):
-        rd = [i] + list(more)
+    def col(k):
+        return ("ff", k, k + 1)
+
+    def fill(o, val):
+        op("v", lambda: v.memset(ap(o), val), [], [o])
+
+    def iota(o, pattern, base=0, cm=0):
+        op("g", lambda: g.iota(ap(o), pattern, base, cm, allow_small_or_imprecise_dtypes=True), [], [o])
+
+    def ts(o, i, s1, op0, s2=None, op1=None):
         if op1 is None:
-            op("v", lambda: v.tensor_scalar(out, in0, s1, None, op0), rd, [o])
+            op("v", lambda: v.tensor_scalar(ap(o), ap(i), ap(s1), None, op0), held(i, s1), [o])
         else:
-            op("v", lambda: v.tensor_scalar(out, in0, s1, s2, op0, op1), rd, [o])
+            op("v", lambda: v.tensor_scalar(ap(o), ap(i), ap(s1), ap(s2), op0, op1), held(i, s1, s2), [o])
 
-    def tt(out, o, in0, i0, in1, i1, opx, more=()):
-        op("v", lambda: v.tensor_tensor(out, in0, in1, opx), [i0, i1] + list(more), [o])
+    def tt(o, i0, i1, opx):
+        op("v", lambda: v.tensor_tensor(ap(o), ap(i0), ap(i1), opx), [i0, i1], [o])
 
-    def copy(out, o, in_, i):
-        op("v", lambda: v.tensor_copy(out, in_), [i], [o])
+    def copy(o, i):
+        op("v", lambda: v.tensor_copy(ap(o), ap(i)), [i], [o])
 
-    def act(out, o, in_, i, func, more=(), **kw):
-        op("a", lambda: sca.activation(out, in_, func, **kw), [i] + list(more), o if isinstance(o, list) else [o])
+    def act(o, i, func, bias=None, scale=None, total=None):
+        kw = {}
+        if bias is not None: kw["bias"] = ap(bias)
+        if scale is not None: kw["scale"] = ap(scale)
+        if total is not None: kw["accum_out"] = ap(total)
+        op("a", lambda: sca.activation(ap(o), ap(i), func, **kw), held(i, bias, scale), held(o, total))
+
+    def const(o, val=0.0):
+        n = len(range(*o[1:]))
+        if isinstance(val, float) and val == 0.0:
+            act(o, ("ident", 0, n), F.Copy, scale=0.0)
+        else:
+            act(o, ("ident", 0, n), F.Identity, bias=val, scale=0.0)
+
+    def gather(q, o, w, l):
+        if q == "v":
+            op("v", lambda: v.tensor_copy(ap(o), ap(w).indirect(ap(l))), [w, l], [o])
+        else:
+            op("a", lambda: sca.activation(ap(o), ap(w).indirect(ap(l)), F.Copy), [w, l], [o])
+
+    def scan(o, d, i):
+        op("v", lambda: v.tensor_tensor_scan(ap(o), ap(d), ap(i), 0.0, A.mult, A.add), [d, i], [o])
+
+    def turn(o, i):
+        op("v", lambda: v.transpose(ap(o), ap(i)), [i], [o])
+
+    def reduce(o, i, opx, **kw):
+        op("v", lambda: v.tensor_reduce(ap(o), ap(i), AxisListType.X, opx, **kw), [i], [o])
 
     def quant(n, c, w, tile, a):
         op("v", lambda: v.quantize_mx(T[n][:, c:c + w], T[n + "s"][:, c:c + w], T[tile][:, a:a + 4 * w]),
            [(tile, a, a + 4 * w)], [(n, c, c + w), (n + "s", c, c + w)])
 
-    def mm(bank, w, ln, l0, rn, r0, start=True, stop=True):
-        op("t", lambda: ten.matmul_mx(ps[:, 512 * bank:512 * bank + w], T[ln][:, l0:l0 + 128], T[ln + "s"][:, l0:l0 + 128],
+    def mm(k, w, ln, l0, rn, r0, start=True, stop=True):
+        op("t", lambda: ten.matmul_mx(T.ps[:, 512 * k:512 * k + w], T[ln][:, l0:l0 + 128], T[ln + "s"][:, l0:l0 + 128],
                                       T[rn][:, r0:r0 + w], T[rn + "s"][:, r0:r0 + w], start, stop),
-           [(ln, l0, l0 + 128), (ln + "s", l0, l0 + 128), (rn, r0, r0 + w), (rn + "s", r0, r0 + w)], [("ps", bank, bank + 1)])
+           [(ln, l0, l0 + 128), (ln + "s", l0, l0 + 128), (rn, r0, r0 + w), (rn + "s", r0, r0 + w)], [bank(k, 0, w)])
 
     def pick(on, o0, sn, w0, w1, ln, e0, e1):
         w = 16 * (e1 - e0)
@@ -228,15 +268,17 @@ def rank_program(g, core, T, topo):
         op("a", lambda: sca.activation(T[on + "s"][:, o0:o0 + w], T[sn + "s"][:, w0:w1].indirect(T[ln][:, e0:e1]), F.Copy),
            [(sn + "s", w0, w1), (ln, e0, e1)], [(on + "s", o0, o0 + w)])
 
-    def bank(k, lo, hi, step=1):
-        return ps[:, 512 * k + lo:512 * k + hi:step]
+    def copyplane(q, dn, d0, sn, s0, w):
+        dma(q, T[dn + "s"][:, d0:d0 + w], T[sn + "s"][:, s0:s0 + w], [(sn + "s", s0, s0 + w)], [(dn + "s", d0, d0 + w)])
 
     def copymx(q, dn, d0, sn, s0, w):
         dma(q, T[dn][:, d0:d0 + w].bitcast(dt.uint8), T[sn][:, s0:s0 + w].bitcast(dt.uint8), [(sn, s0, s0 + w)], [(dn, d0, d0 + w)])
-        dma(q, T[dn + "s"][:, d0:d0 + w], T[sn + "s"][:, s0:s0 + w], [(sn + "s", s0, s0 + w)], [(dn + "s", d0, d0 + w)])
+        copyplane(q, dn, d0, sn, s0, w)
 
-    def zeros(n, lo, hi):
-        dma("s", T[n][:, lo:hi], T.zt[:, Z0:Z0 + hi - lo], [("zt", Z0, Z0 + hi - lo)], [(n, lo, hi)])
+    def store(lo, hi):
+        dma("s", T.oc[:, 4 * lo:4 * hi], T.eo[:, lo:hi].bitcast(dt.uint8), [("eo", lo, hi)], [("oc", lo, hi)])
+        for k in range(4):
+            dma("s", T.osc[4 * k:4 * k + 4, lo:hi], T.eos[32 * k:32 * k + 4, lo:hi], [("eos", lo, hi)], [("osc%d" % k, lo, hi)])
 
     def load(q, dst, src, k):
         sl = slice(4 * PW * k, 4 * PW * k + 4 * PW)
@@ -248,64 +290,50 @@ def rank_program(g, core, T, topo):
     load("a", "gt", "gr", 1)
     load("s", "et", "er", 2)
     load("a", "gt", "gr", 2)
-    dma("s", T.ft[:, 0:192], T.fo[:, 0:192], [], [("ft", 0, 192)])
-    dma("s", T.wt[:, 0:512], T.w[:, 0:512], [], [("wt", 0, 512)])
 
     op("g", lambda: g.iota(T.pidx[:, 0:1], [[0, 1]], 0, 1), [], [("pidx", 0, 4)])
-    fill("ones", 0, 520, 1.0)
-    select("ident", 0, 516, "ones", 516, [[-1, 516]], A.is_equal, 3, 4)
-    iota("r3", 3, [[128, 3]])
-    iota("r6", 6, [[128, 3], [1, 2]])
-    iota("jrowe", 512, [[0, 8], [1, 16], [64, 4]])
-    iota("row144", 144, [[-16, 3], [1, 48]])
-    jrow = T.jrowe[:, 0:512:4]
+    iota(("pj", 0, 128), [[1, 128]], 0, -1)
+    iota(("row", 0, 144), [[-16, 3], [1, 48]])
+    iota(("jr", 0, 128), [[0, 8], [1, 16]])
+    jr = ("jr", 0, 128)
 
-    def ibit(k, s1, s2, op0, op1=None):
-        ts(T.ii[:, k:k + 1], ("ii", k, k + 1), T.pidx[:, 0:1], ("pidx", 0, 4), s1, s2, op0, op1)
+    def ibit(k, s1, op0, s2=None, op1=None):
+        ts(("ii", k, k + 1), ("pidx", 0, 1), s1, op0, s2, op1)
+    fill(("ident", 0, 520), 0.0)
+    ibit(0, 15, A.bitwise_and)
+    ibit(1, 4, A.logical_shift_right)
+    ibit(2, 4, A.logical_shift_right, 14, A.bitwise_and)
+    ibit(3, 2, A.logical_shift_right, 3, A.bitwise_and)
+    copy(("ff", 0, 4), ("ii", 0, 4))
+    ts(("ident", 3, 515, 4), ("pj", 0, 128), 0.0, A.is_equal)
+    ts(col(9), col(1), float(rank), A.is_equal)
 
-    def col(k):
-        return T.ff[:, k:k + 1]
-
-    def fc(k, src, s1, s2, op0, op1, more=()):
-        ts(col(k), ("ff", k, k + 1), col(src), ("ff", src, src + 1), s1, s2, op0, op1, [("ff", m, m + 1) for m in more])
-    ibit(0, 15, None, A.bitwise_and)
-    ibit(1, 4, None, A.logical_shift_right)
-    ibit(2, 4, 14, A.logical_shift_right, A.bitwise_and)
-    ibit(3, 1, None, A.bitwise_and)
-    ibit(4, 15, 1, A.bitwise_and, A.logical_shift_right)
-    copy(T.ii[:, 5:6], ("ii", 5, 6), T.pidx[:, 0:1], ("pidx", 0, 4))
-    ibit(6, 7, None, A.bitwise_and)
-    copy(T.ff[:, 0:7], ("ff", 0, 7), T.ii[:, 0:7], ("ii", 0, 7))
-    fc(9, 1, float(rank), None, A.is_equal, None)
-    fill("zt", 0, 616, 0.0)
-    fc(16, 0, 8.0, col(1), A.mult, A.add, [1])
-    fc(17, 0, 8.0, col(2), A.mult, A.add, [2])
-    ts(T.ii[:, 8:9], ("ii", 8, 9), col(16), ("ff", 16, 17), 16.0, None, A.add)
-    ts(T.ii[:, 9:10], ("ii", 9, 10), T.ii[:, 8:9], ("ii", 8, 9), 480, None, A.bitwise_and)
-    copy(col(21), ("ff", 21, 22), T.ii[:, 9:10], ("ii", 9, 10))
-    fc(20, 16, col(21), None, A.subtract, None, [21])
-    fill("hh", 512, 528, 0.0)
-    op("v", lambda: v.memset(T.hh[:, 3:512:4], 0.0), [], [("hh", 0, 512, 4, 3)])
-    for b in range(4):
-        quant("ce", 128 * b, 128, "ident", 3 - b)
-
-    act(T.own[:, 0:48], ("own", 0, 48), T.ones[:, 0:48], ("ones", 0, 48), F.Copy, scale=99.0)
+    const(("ow1", 0, 512), col(9))
+    for h in range(2):
+        op("g", lambda: g.affine_select(T.slt[:, 512 * h:512 * h + 512], T.ow1[:, 0:512], [[0, 4], [-2, 32], [16, 4]], A.is_equal, 0.0, -16 * rank - h, 1),
+           [("ow1", 0, 512)], [("slt", 512 * h, 512 * h + 512)])
+    iota(("st3", 0, 520), [[0, 520]])
+    const(("own", 0, 48), 99.0)
+    act(col(16), col(0), F.Identity, col(1), 8.0)
     for t in range(4):
         for k, o in ((3 * t, units[t][0]), (3 * t + 2, units[t][1])):
-            act(T.own[:, 4 * k:4 * k + 4], ("own", 4 * k, 4 * k + 4), T.ones[:, 0:4], ("ones", 0, 4), F.Copy, scale=float(o))
-    act(T.kc[:, 0:1], ("kc", 0, 1), T.ones[:, 0:1], ("ones", 0, 1), F.Copy, scale=-15.5)
-    act(T.kc[:, 1:2], ("kc", 1, 2), T.ones[:, 0:1], ("ones", 0, 1), F.Copy, scale=-1800.0)
-    act(T.ow2[:, 0:48], ("ow2", 0, 48), T.own[:, 0:48], ("own", 0, 48), F.Abs, [("ff", 1, 2)], bias=col(1), scale=-1.0)
-    act(T.ow3[:, 0:48], ("ow3", 0, 48), T.ow2[:, 0:48], ("ow2", 0, 48), F.Relu, [("ones", 0, 1)], bias=T.ones[:, 0:1], scale=-1.0)
-    act(T.ow1[:, 0:512], ("ow1", 0, 512), T.ones[:, 0:512], ("ones", 0, 512), F.Copy, [("ff", 9, 10)], scale=col(9))
-    act(T.kc[:, 2:3], ("kc", 2, 3), col(0), ("ff", 0, 1), F.Copy, scale=TINY)
-    act(T.kc[:, 3:4], ("kc", 3, 4), col(5), ("ff", 5, 6), F.Copy, scale=TINY)
+            const(("own", 4 * k, 4 * k + 4), float(o))
+    act(col(27), col(3), F.Identity, 128.0, 32.0)
+    act(("ow2", 0, 48), ("own", 0, 48), F.Abs, col(1), -1.0)
+    act(col(21), col(16), F.Identity, 112.0)
+    act(("ff", 22, 25), ("row", 0, 3), F.Identity, col(27), 128.0)
+    act(("ow3", 0, 48), ("ow2", 0, 48), F.Relu, 1.0, -1.0)
+    act(col(20), col(27), F.Identity, col(21), -1.0)
     for e in range(4):
-        act(T.ur[:, e:512:4], ("ur", 0, 512, 4, e), T.zt[:, Z0:Z0 + 128], ("zt", Z0, Z0 + 128), F.Identity, [("ut", 0, 8)], bias=T.ut[:, e:e + 1])
-    act(T.thr[:, 0:144], ("thr", 0, 144), T.row144[:, 0:144], ("row144", 0, 144), F.Relu, [("kc", 2, 3)], bias=T.kc[:, 2:3], scale=-TINY)
-    for h in range(2):
-        select("slt", 512 * h, 512 * h + 512, "ow1", 512, [[0, 4], [-2, 32], [16, 4]], A.is_equal, -16 * rank - h, 1)
-    select("st", 1024, 1536, "ones", 512, [[0, 8], [-1, 16], [-256, 4]], A.is_equal, 512 - 16 * rank, 1)
+        act(("ur", e, 512, 4), ("pj", 0, 128), F.Identity, ("ut", e, e + 1), 0.0)
+    const(("zt", 0, 512))
+    act(col(17), col(0), F.Identity, col(2), 8.0)
+    act(col(10), col(2), F.Identity, col(1), -1.0)
+    for c in range(3):
+        act(("zt", c, 48, 4), ("ow3", c, 48, 4), F.Copy, scale=col(22 + c))
+    act(("zt", 48, 96), ("ow3", 0, 48), F.Copy, scale=col(20))
+    act(col(12), col(10), F.Identity, col(17), 128.0)
+    const(("zt", 512, 768))
 
     BE = ((0, 1, 2, 3), (4, 5, 6, 7), (0, 1, 2, 4))
     BS = (3, 5, 6)
@@ -316,93 +344,87 @@ def rank_program(g, core, T, topo):
             mm(BE[k][b], PW, "ce", 128 * b, "qe", PW * k)
 
     def values(k, b):
-        lo, hi = 4 * PW * k, 4 * PW * k + 4 * PW
-        sl = slice(lo + b, hi, 4)
-        n = BE[k][b]
-        tt(T.h[:, sl], ("h", lo, hi, 4, b), bank(n, 0, PW), ("ps", n, n + 1), T.gt[:, sl], ("gt", lo, hi), A.add)
+        lo, hi = 4 * PW * k + b, 4 * PW * k + 4 * PW
+        tt(("h", lo, hi, 4), bank(BE[k][b], 0, PW), ("gt", lo, hi, 4), A.add)
 
     def codes_of(k):
         quant("qq", Q0 + PW * k, PW, "h", 4 * PW * k)
 
     def scores(k):
-        n = BS[k]
-        mm(n, PW, "cu", 0, "qq", Q0 + PW * k)
-        act(T.zs[:, PW * k:PW * k + PW], ("zs", PW * k, PW * k + PW), bank(n, 0, PW), ("ps", n, n + 1), F.Abs)
+        mm(BS[k], PW, "cu", 0, "qq", Q0 + PW * k)
+        act(("zs", PW * k, PW * k + PW), bank(BS[k], 0, PW), F.Abs)
+    for b in range(4):
+        quant("ce", 128 * b, 128, "ident", 3 - b)
     errors(0)
-    ts(T.ff[:, 22:25], ("ff", 22, 25), T.r3[:, 0:3], ("r3", 0, 3), col(21), 128.0, A.add, A.add, [("ff", 21, 22)])
-    ts(T.goff[:, 0:3], ("goff", 0, 3), T.r3[:, 0:3], ("r3", 0, 3), col(16), None, A.add, None, [("ff", 16, 17)])
-    ts(T.goff[:, 3:9], ("goff", 3, 9), T.r6[:, 0:6], ("r6", 0, 6), col(17), None, A.add, None, [("ff", 17, 18)])
-    for c in range(3):
-        act(T.zt[:, c:48:4], ("zt", 0, 48, 4, c), T.ow3[:, c:48:4], ("ow3", 0, 48), F.Copy, [("ff", 22 + c, 23 + c)], scale=col(22 + c))
-    act(T.zt[:, 48:96], ("zt", 48, 96), T.ow3[:, 0:48], ("ow3", 0, 48), F.Copy, [("ff", 20, 21)], scale=col(20))
-
-    def pattern(c, bias, rd):
-        o = 512 * c
-        act(T.stt[:, o:o + 512], ("stt", o, o + 512), T.jrowe[:, 0:512], ("jrowe", 0, 512), F.Abs, rd, bias=bias, scale=-1.0)
-        act(T.st[:, o:o + 512], ("st", o, o + 512), T.stt[:, o:o + 512], ("stt", o, o + 512), F.Relu, [("ff", 9, 10)], bias=col(9), scale=-1.0)
-    pattern(0, col(0), [("ff", 0, 1)])
-    quant("cu", 0, 128, "ur", 0)
+    ibit(4, 1, A.bitwise_and)
+    ibit(5, 15, A.bitwise_and, 1, A.logical_shift_right)
+    ibit(6, 7, A.bitwise_and)
     values(0, 0)
     values(0, 1)
     errors(1)
     values(0, 2)
     values(0, 3)
-    codes_of(0)
     values(1, 0)
+    codes_of(0)
     values(1, 1)
     errors(2)
     values(1, 2)
     values(1, 3)
+    quant("cu", 0, 128, "ur", 0)
     codes_of(1)
     scores(0)
     scores(1)
+    act(col(28), col(0), F.Copy, scale=TINY)
+    const(("d0", 0, 144), 1.0)
+    act(("thr", 0, 144), ("row", 0, 144), F.Relu, col(28), -TINY)
+    const(("d0", 0, 144, 48))
     for b in range(4):
         values(2, b)
+    ts(("goff", 0, 3), ("row", 0, 3), 128.0, A.mult, col(16), A.add)
     codes_of(2)
     scores(2)
     for b in range(2):
         mm(b, 384, "ce", 128 * b, "qq", Q0)
-    before("s", [("et", 1024, 1536)])
-    for k in range(3):
-        zeros("fxt", 512 * k, 512 * k + 512)
-    zeros("oht", 0, 512)
-    zeros("l2t", 0, 512)
-    zeros("at", 384, 512)
-    zeros("x2", 0, 512)
-    zeros("lt", 192, 512)
-    copymx("s", "pb", B, "ce", 0, 128 - B)
-    fill("d0", 0, 144, 1.0)
-    fill("d0", 0, 144, 0.0, 48)
+    before("s", [("gt", 1024, 1536)])
+    dma("s", T.ft[:, 0:192], T.fo[:, 0:192], [], [("ft", 0, 192)])
+    copyplane("s", "sc", 0, "ce", 0, S0)
+    dma("s", T.wt[:, 0:512], T.w[:, 0:512], [], [("wt", 0, 512)])
+    ts(("goff", 3, 4), col(17), 257.0, A.add)
+    ts(("goff", 4, 6), ("row", 0, 2), col(12), A.add)
     quant("ce", CW, 140, "zt", 0)
-    fc(11, 0, 64.0, None, A.add, None)
+    quant("land2", 0, ZC, "zt", 4 * WZ)
+    copymx("s", "land", ZC, "ce", CW + WZ, 2)
     second = [u for u in units if rank in u][0][1] == rank
     lp, dlt = (0, 1) if second else (K, 0)
-    fc(18, 6, float(SEG), float(dlt), A.mult, A.add)
 
-    op("v", lambda: v.tensor_copy(T.zg[:, 0:144], T.zs[:, 0:384].indirect(T.goff[:, 0:9])), [("zs", 0, 384), ("goff", 0, 9)], [("zg", 0, 144)])
-    op("v", lambda: v.transpose(T.zt2[:, 0:96], T.zg[:, 48:144]), [("zg", 48, 144)], [("zt2", 0, 96)])
+    gather("v", ("zg", 0, 96), ("zs", 0, 384), ("goff", 0, 6))
+    const(("hh", 512, 528))
+    const(("hh", 3, 512, 4))
+    copy(("ff", 4, 7), ("ii", 4, 7))
+    turn(("zt2", 0, 64), ("zg", 32, 96))
+    ts(col(26), col(1), 2.5, A.is_lt)
+    for c, x in ((0, 32), (1, 48)):
+        ts(("tt", 48 * c, 48 * c + 48), ("zg", 0, 48), ("zt2", x, x + 1), A.subtract, -1.0, A.mult)
+    act(("tt", 96, 144), ("zg", 0, 48), F.Identity, ("zt2", 0, 1), -1.0)
+    const(("fxt", 0, 384))
+    tt(("bb", 0, 144), ("tt", 0, 144), ("thr", 0, 144), A.is_lt)
+    scan(("cum", 0, 144), ("d0", 0, 144), ("bb", 0, 144))
+    ranks = ("cum", 47, 144, 48)
+    act(("t4", 0, 3), ranks, F.Identity, -3600.0, 240.0)
     for c in range(3):
-        ts(T.tt[:, 48 * c:48 * c + 48], ("tt", 48 * c, 48 * c + 48), T.zg[:, 0:48], ("zg", 0, 48), T.zt2[:, 32 * c:32 * c + 1], -1.0, A.subtract, A.mult, [("zt2", 0, 96)])
-    tt(T.bb[:, 0:144], ("bb", 0, 144), T.tt[:, 0:144], ("tt", 0, 144), T.thr[:, 0:144], ("thr", 0, 144), A.is_lt)
-    op("v", lambda: v.tensor_tensor_scan(T.cum[:, 0:144], T.d0[:, 0:144], T.bb[:, 0:144], 0.0, A.mult, A.add), [("d0", 0, 144), ("bb", 0, 144)], [("cum", 0, 144)])
-    act(T.t3[:, 0:3], ("t3", 0, 3), T.cum[:, 47:144:48], ("cum", 0, 144), F.Sign, [("kc", 0, 1)], bias=T.kc[:, 0:1])
-    act(T.t4[:, 0:3], ("t4", 0, 3), T.t3[:, 0:3], ("t3", 0, 3), F.Copy, scale=240.0)
-    for c in range(3):
-        ts(T.hh[:, c:512:4], ("hh", 0, 512, 4, c), jrow, ("jrowe", 0, 512), T.cum[:, 48 * c + 47:48 * c + 48], None, A.is_equal, None, [("cum", 0, 144)])
-    tt(T.hh[:, 512:515], ("hh", 512, 515), T.t4[:, 0:3], ("t4", 0, 3), T.cum[:, 47:144:48], ("cum", 0, 144), A.max)
-    quant("qq", 0, 132, "hh", 0)
+        ts(("hh", c, 512, 4), jr, ("cum", 48 * c + 47, 48 * c + 48), A.is_equal)
+    tt(("hh", 512, 515), ("t4", 0, 3), ranks, A.max)
+    quant("qq", H0, 132, "hh", 0)
     for k in range(2):
-        mm(2, 128, "qq", 0, "ce", CW + 12 * k, k == 0, k == 1)
+        mm(2, 128, "qq", H0, "ce", CW + 12 * k, k == 0, k == 1)
     mm(7, 384, "ce", 256, "qq", Q0)
     mm(3, 384, "ce", 384, "qq", Q0)
-
-    def left_over(b, n):
-        sl = slice(b, 1536, 4)
-        tt(T.lf[:, sl], ("lf", 0, 1536, 4, b), T.h[:, sl], ("h", 0, 1536), bank(n, 0, 384), ("ps", n, n + 1), A.subtract)
-    left_over(0, 0)
-    ts(T.off1[:, 0:12], ("off1", 0, 12), bank(2, 0, 12), ("ps", 2, 3), float(L0), None, A.add)
-    pick("sc", 0, "qq", 0, 640, "off1", 0, 6)
-    pick("sc", 96, "qq", 0, 640, "off1", 6, 12)
+    quant("ce", SL, 256, "slt", 0)
+    ts(("off1", 0, 12), bank(2, 0, 12), float(L0 - 128), A.add)
+    const(("fxt", 384, 896))
+    act(("t3", 0, 3), ranks, F.Sign, -15.5)
+    pick("sc", S0, "qq", 128, 640, "off1", 0, 6)
+    pick("sc", S0 + 96, "qq", 128, 640, "off1", 6, 12)
 
     def did(d):
         rid, pid = topo.addr(d, core)
@@ -415,60 +437,76 @@ def rank_program(g, core, T, topo):
     half = len(hop) // 2
     run = {}
     for t in range(4):
-        run[units[t][0]] = (48 * t, 48 * t + SEG)
-        run[units[t][1]] = (48 * t + 48 - SEG, 48 * t + 48)
+        run[units[t][0]] = S0 + B * t
+        run[units[t][1]] = S0 + B * t + B - SEG
     me = (SEG * rank, SEG * rank + SEG)
-    left = [0]
-    for codes, hs in ((True, far), (False, near)):
-        nm = "sc" if codes else "scs"
-        before("g", [(nm, 0, 96)])
-        g.remote_dma_fused([RemoteDMATransfer(dst_ids=[did(hs[t])], dma_engine_mask=bits(hop[half * t:half * t + half]), remote_sem=T.sem.h1,
-                                              srcs=[mxv("sc", 48 * t, 48 * t + 48, codes)], dsts=[mxv("hc", 0, 48, codes)]) for t in range(2)], local_sem=T.sem.ls)
-        left[0] += 2 * half
+    before("g", [("sc", S0, S0 + 96), ("scs", 0, S0 + 96), ("land2", 0, ZC), ("land2s", 0, ZC)])
+    g.remote_dma_fused(
+        [RemoteDMATransfer(dst_ids=[did(far[t])], dma_engine_mask=bits(hop[half * t:half * t + half]), remote_sem=T.sem.h1,
+                           srcs=[mxv("sc", S0 + B * t, S0 + B * t + B, True)], dsts=[mxv("hc", 0, B, True)]) for t in range(2)] +
+        [RemoteDMATransfer(dst_ids=[did(near[t])], dma_engine_mask=bits(off[half * t:half * t + half]), remote_sem=T.sem.h1,
+                           srcs=[mxv("sc", 0, 4 * B, False)], dsts=[mxv("hc", 0, 4 * B, False)]) for t in range(2)], local_sem=T.sem.ls1)
     for codes in (True, False):
-        nm = "sc" if codes else "scs"
-        before("g", [(nm, 96, 192)])
-        tr = []
-        for j in range(3):
-            r = T.rank_of(direct[j])
-            es = split(off, j, not codes)
-            tr.append(RemoteDMATransfer(dst_ids=[did(direct[j])], dma_engine_mask=bits(es), remote_sem=T.sem.arr1,
-                                        srcs=[mxv("sc", run[r][0], run[r][1], codes)], dsts=[mxv("land", me[0], me[1], codes)]))
-            left[0] += len(es)
-        g.remote_dma_fused(tr, local_sem=T.sem.ls)
-    copymx("s", "land", me[0], "sc", run[rank][0], SEG)
-    copymx("s", "land", ZC, "qq", 130, 2)
-    iota("r3b", 3, [[16, 3]])
-    iota("row48", 48, [[1, 48]])
-    select("dx", 0, 384, "ones", 384, [[0, 48], [1, 8]], A.not_equal, 0, 0)
-    iota("mkrow", 72, [[-8, 3], [1, 24]])
-    iota("row16k", 24, [[16, 24]])
+        before("g", [("sc" if codes else "scs", S0 + 96, S0 + 192)])
+        g.remote_dma_fused([RemoteDMATransfer(dst_ids=[did(direct[j])], dma_engine_mask=bits(split(off, j, not codes)), remote_sem=T.sem.arr1,
+                                              srcs=[mxv("sc", run[T.rank_of(direct[j])], run[T.rank_of(direct[j])] + SEG, codes)],
+                                              dsts=[mxv("land", me[0], me[1], codes)]) for j in range(3)], local_sem=T.sem.ls1)
+    arrive("ls1", len(hop) + 3 * len(off), [("gone1", 0, 1)])
+    copymx("s", "land", me[0], "sc", run[rank], SEG)
+    iota(("al", 192, 704), [[0, 512]])
+    iota(("oht", 0, 512), [[0, 512]])
 
+    def left_over(b, n):
+        tt(("lf", b, 1536, 4), ("h", b, 1536, 4), bank(n, 0, 384), A.subtract)
+    const(("fxt", 896, 1408))
+    const(("fxt", 1408, 1536))
+    act(("s3", 0, 3), ("t3", 0, 3), F.Identity, 0.5, -0.5)
+    act(col(19), col(4), F.Identity, col(1), 8.0)
     for e in range(4):
-        act(T.fxt[:, e:1536:32], ("fxt", 0, 1536, 32, e), T.ft[:, e:192:4], ("ft", 0, 192), F.Copy)
-    pattern(1, col(11), [("ff", 11, 12)])
-    left_over(1, 1)
+        act(("fxt", e, 1536, 32), ("ft", e, 192, 4), F.Copy)
+    act(("xa", 0, 48), ("row", 48, 96), F.Abs, col(5), -1.0)
+    act(("xb", 0, 3), ("row", 0, 3), F.Abs, col(1), -1.0)
+    act(col(25), col(26), F.Copy, scale=16.0)
+    for c in range(3):
+        act(("zt", 4 * WX + c, 4 * WE, 4), ("xa", 16 - 8 * c, 40 - 8 * c), F.Relu, float(P), -float(P))
+    act(("zt", 4 * WE + 1, 4 * WE + 13, 4), ("xb", 0, 3), F.Relu, 128.0, -128.0)
+    act(("zt", 4 * WN, 4 * WN + 1), col(1), F.Copy, scale=col(25))
+    act(("zt", 4 * WN + 4, 4 * WN + 5), col(0), F.Copy, scale=col(26))
+    act(("sta", 0, 128), jr, F.Abs, col(0), -1.0)
+    act(("nk", 0, 24), ("row", 0, 24), F.Identity, col(0), 16.0)
+    act(("st3", 3, 515, 4), ("sta", 0, 128), F.Relu, col(9), -1.0)
+    left_over(2, 7)
+    left_over(3, 3)
+    left_over(0, 0)
     quant("fx", 0, 384, "fxt", 0)
-    quant("ce", SL, 256, "slt", 0)
     BD = (4, 5, 6)
     for b in range(3):
         mm(BD[b], 384, "ce", 128 * b, "fx", 0, True, False)
-    left_over(2, 7)
-    left_over(3, 3)
-    for k, n in ((0, 7), (1, 3)):
-        mm(n, 192, "ce", 384, "fx", 192 * k, True, False)
+    mm(7, 256, "ce", 384, "fx", 0, True, False)
+    mm(3, 128, "ce", 384, "fx", 256, True, False)
+    for c in range(3):
+        ts(("hh", c, 512, 4), jr, col(19), A.is_equal, ("s3", c, c + 1), A.mult)
+    ts(col(18), col(6), float(SEG), A.mult, float(dlt), A.add)
+    quant("c2", 0, 128, "hh", 0)
+    quant("ce", CX, WALL - WN, "zt", 4 * WN)
+    mm(2, 128, "c2", 0, "ce", CX + WX - WN)
+    left_over(1, 1)
+    tt(("tq2", 0, 24), bank(2, 0, 24), ("nk", 0, 24), A.add)
     quant("qq", E0, 384, "lf", 0)
-    ts(T.mc[:, 0:3], ("mc", 0, 3), T.r3b[:, 0:3], ("r3b", 0, 3), col(0), None, A.add, None, [("ff", 0, 1)])
-    ts(T.m2[:, 0:3], ("m2", 0, 3), T.mc[:, 0:3], ("mc", 0, 3), 2.0, 0.5, A.mult, A.add)
-    quant("ce", CS3, 384, "st", 0)
-    fc(25, 1, 2.5, 16.0, A.is_lt, A.mult)
-    fc(26, 1, 2.5, None, A.is_lt, None)
-    fill("l2t", 2, 3, float(rank))
+    copy(("off3", 0, 24), ("tq2", 0, 24))
+    for c in range(3):
+        quant("ce", CS3 + 128 * c, 128, "st3", 3 - c)
+    const(("dx", 0, 384), 1.0)
     for e in range(4):
-        act(T.at[:, 4 + e:384:8], ("at", 0, 384, 8, 4 + e), T.ft[:, e:192:4], ("ft", 0, 192), F.Copy)
-    act(T.zt[:, WN:WN + 1], ("zt", WN, WN + 1), col(1), ("ff", 1, 2), F.Copy, [("ff", 25, 26)], scale=col(25))
-    act(T.zt[:, WN + 4:WN + 5], ("zt", WN + 4, WN + 5), col(0), ("ff", 0, 1), F.Copy, [("ff", 26, 27)], scale=col(26))
-    act(T.thr2[:, 0:48], ("thr2", 0, 48), T.row48[:, 0:48], ("row48", 0, 48), F.Relu, [("kc", 3, 4)], bias=T.kc[:, 3:4], scale=-TINY)
+        act(("so", SW * e, SW * e + B), ("ft", e, 192, 4), F.Copy)
+    const(("dx", 0, 384, 8))
+    act(col(29), ("pj", 0, 1), F.Copy, scale=-TINY)
+    act(("sa", 0, 3), ("nk", 0, 3), F.Identity, -27.5, -3.5)
+    act(("ba", 0, 3), ("nk", 0, 3), F.Identity, 27.5, 4.5)
+    act(("thr2", 0, 48), ("row", 0, 48), F.Relu, col(29), -TINY)
+    pick("eo", 0, "qq", Q0, 1024, "off3", 0, 24)
+    before("s", [("gone1", 0, 1)])
+    store(0, P)
 
     total = 0
     for s in range(8):
@@ -483,129 +521,115 @@ def rank_program(g, core, T, topo):
             total += len(off)
     arrive("arr1", total, [(n, SEG * s, SEG * s + SEG) for s in range(8) if s != rank for n in ("land", "lands")])
     for h in range(2):
-        mm(h, 8 * SEG, "ce", SL + 128 * h, "land", 0)
+        mm(h, ZC, "ce", SL + 128 * h, "land", 0)
     for k in range(2):
-        copy(T.tin[:, 16 * k:16 * k + 8], ("tin", 16 * k, 16 * k + 8), bank(0, lp, ZC, SEG), ("ps", 0, 1))
-        act(T.tin[:, 16 * k + 8:16 * k + 16], ("tin", 16 * k + 8, 16 * k + 16), bank(1, lp, ZC, SEG), ("ps", 1, 2), F.Copy)
-    op("v", lambda: v.transpose(T.tto[:, 0:32], T.tin[:, 0:32]), [("tin", 0, 32)], [("tto", 0, 32)])
-    ts(T.off4[:, 0:24], ("off4", 0, 24), T.tto[:, 0:24], ("tto", 0, 32), col(18), float(ZC), A.add, A.min, [("ff", 18, 19)])
-    for k in range(2):
-        pick("pq", 192 * k, "land", 0, LW, "off4", 12 * k, 12 * k + 12)
+        act(("tin", 16 * k, 16 * k + 8), bank(0, lp, ZC, SEG), F.Copy)
+        copy(("tin", 16 * k + 8, 16 * k + 16), bank(1, lp, ZC, SEG))
     for c in range(3):
-        mm((2, 0, 1)[c], 8 * SEG, "ce", CS3 + 128 * c, "land", 0)
-    mm(7, 192, "ce", 384, "pq", 0, False, True)
+        mm((2, 0, 1)[c], ZC, "ce", CS3 + 128 * c, "land", 0)
+        act(("junk", 8 * c, 8 * c + 8), bank((2, 0, 1)[c], lp, ZC, SEG), F.Sign, -100.0, total=("sm", c, c + 1))
+    turn(("tto", 0, 32), ("tin", 0, 32))
+    ts(("off4", 0, 24), ("tto", 0, 24), col(18), A.add, float(ZC), A.min)
+    pick("pq", 0, "land", 0, LW, "off4", 0, 16)
+    pick("pq", 256, "land", 0, LW, "off4", 16, 24)
+    mm(7, 256, "ce", 384, "pq", 0, False, True)
     for b in range(3):
         mm(BD[b], 384, "ce", 128 * b, "pq", 0, False, True)
-    mm(3, 192, "ce", 384, "pq", 192, False, True)
+    mm(3, 128, "ce", 384, "pq", 256, False, True)
+    act(("pf", 0, 3), ("sm", 0, 3), F.Sign, -7.0)
+    at, window = winners_at(rank)
+    nat = 508 if at else 192
+    const(("al", nat + 2, nat + 3), float(rank))
     for c in range(3):
-        k = (2, 0, 1)[c]
-        act(T.junk[:, 0:8], [("junk", 0, 8), ("sm", c, c + 1)], bank(k, lp, ZC, SEG), ("ps", k, k + 1), F.Copy, accum_out=T.sm[:, c:c + 1])
-    act(T.pf[:, 0:3], ("pf", 0, 3), T.sm[:, 0:3], ("sm", 0, 3), F.Sign, [("kc", 1, 2)], bias=T.kc[:, 1:2])
-    for c in range(3):
-        act(T.pg[:, c:c + 1], ("pg", c, c + 1), T.pf[:, c:c + 1], ("pf", 0, 3), F.Identity, [("m2", 0, 3)], bias=T.m2[:, c:c + 1], scale=0.5)
+        act(("pg", c, c + 1), ("pf", c, c + 1), F.Identity, ("ba", c, c + 1), ("sa", c, c + 1))
 
     def sums(b, lo, hi, n):
-        o = 384 * b
-        op("v", lambda: v.tensor_tensor_scan(T.so[:, o + lo:o + hi], T.dx[:, 0:hi - lo], bank(n, 0, hi - lo), 0.0, A.mult, A.add),
-           [("dx", 0, 384), ("ps", n, n + 1)], [("so", o + lo, o + hi)])
+        scan(("so", SW * b + B + lo, SW * b + B + hi), ("dx", 0, hi - lo), bank(n, 0, hi - lo))
 
-    def summed(q, b, lo, hi):
-        o = 384 * b
-        out, in_ = T.at[:, lo + b:hi:8], T.so[:, o + lo + 7:o + hi:8]
-        if q == "a":
-            act(out, ("at", lo, hi, 8, b), in_, ("so", o + lo, o + hi), F.Copy)
-        else:
-            copy(out, ("at", lo, hi, 8, b), in_, ("so", o + lo, o + hi))
-    sums(3, 0, 192, 7)
-    summed("a", 3, 0, 192)
-    quant("ce", CWN, 128, "zt", WN)
-    fc(27, 1, 128.0, None, A.mult, None)
-    ts(T.m3[:, 0:3], ("m3", 0, 3), T.r3[:, 0:3], ("r3", 0, 3), col(27), 15.5, A.is_equal, A.mult, [("ff", 27, 28)])
-    fc(19, 3, 8.0, col(1), A.mult, A.add, [1])
+    def summed(e, b, lo, hi):
+        gather(e, ("al", 64 * lo + b, 64 * hi, 4), ("so", SW * b, SW * b + B + 128 * hi), ("plist", lo, hi))
+    sums(3, 0, 256, 7)
     sums(0, 0, 384, 4)
-    summed("a", 0, 0, 384)
+    copy(("plist", 0, 3), ("pg", 0, 3))
+    summed("a", 3, 0, 2)
+    summed("a", 0, 0, 3)
     sums(1, 0, 384, 5)
-    summed("a", 1, 0, 384)
-    copy(T.plist[:, 0:3], ("plist", 0, 3), T.pg[:, 0:3], ("pg", 0, 3))
+    summed("a", 1, 0, 3)
     sums(2, 0, 384, 6)
-    summed("a", 2, 0, 384)
-    sums(3, 192, 384, 3)
-    summed("v", 3, 192, 384)
-    quant("pa", 0, 128, "at", 0)
-    pick("pb", 0, "pa", 0, 128, "plist", 0, 3)
+    summed("a", 2, 0, 3)
+    sums(3, 256, 384, 3)
+    summed("v", 3, 2, 3)
+    quant("pb", 0, 128, "al", 0)
 
     mm(1, 128, "cu", 0, "pb", 0)
     mm(0, 128, "pb", 0, "cu", 0)
-    act(T.zab[:, 0:48], ("zab", 0, 48), bank(1, 0, 48), ("ps", 1, 2), F.Abs)
-    for e in range(3):
-        ts(T.ste[:, e:512:4], ("ste", 0, 512, 4, e), jrow, ("jrowe", 0, 512), col(19), None, A.is_equal, None, [("ff", 19, 20)])
-    ts(T.ste[:, 3:512:4], ("ste", 0, 512, 4, 3), jrow, ("jrowe", 0, 512), col(0), None, A.is_equal, None, [("ff", 0, 1)])
-    op("v", lambda: v.tensor_reduce(T.zca[:, 0:1], bank(0, 0, 1), AxisListType.X, A.max, apply_absolute_value=True), [("ps", 0, 1)], [("zca", 0, 1)])
-    ts(T.tq[:, 0:48], ("tq", 0, 48), T.zab[:, 0:48], ("zab", 0, 48), T.zca[:, 0:1], -1.0, A.subtract, A.mult, [("zca", 0, 1)])
-    tt(T.bt[:, 0:48], ("bt", 0, 48), T.tq[:, 0:48], ("tq", 0, 48), T.thr2[:, 0:48], ("thr2", 0, 48), A.is_lt)
-    op("v", lambda: v.tensor_reduce(T.rk[:, 0:1], T.bt[:, 0:48], AxisListType.X, A.add), [("bt", 0, 48)], [("rk", 0, 1)])
-    ts(T.oht[:, 0:512:4], ("oht", 0, 512, 4, 0), jrow, ("jrowe", 0, 512), T.rk[:, 0:1], None, A.is_equal, None, [("rk", 0, 1)])
+    act(("zab", 0, 48), bank(1, 0, 48), F.Abs)
+    for e in range(4):
+        act(("st2", e, 512, 4), ("ident", 3, 515, 4), F.Copy, scale=(8.0, 8.0, 1.0, 0.0)[e])
+    quant("qw", 0, 128, "wt", 0)
+    reduce(("zca", 0, 1), bank(0, 0, 1), A.max, apply_absolute_value=True)
+    ts(("tq", 0, 48), ("zab", 0, 48), ("zca", 0, 1), A.subtract, -1.0, A.mult)
+    tt(("bt", 0, 48), ("tq", 0, 48), ("thr2", 0, 48), A.is_lt)
+    reduce(("rk", 0, 1), ("bt", 0, 48), A.add)
+    ts(("oht", 0, 512, 4), jr, ("rk", 0, 1), A.is_equal)
     quant("cbt", 0, 128, "oht", 0)
-    mm(2, 128, "cbt", 0, "ce", CWN)
-    quant("ce", CSE, 128, "ste", 0)
-    ts(T.wl[:, 0:1], ("wl", 0, 1), bank(2, 0, 1), ("ps", 2, 3), bank(2, 1, 2), None, A.add, None)
-    copy(T.l2t[:, 0:2], ("l2t", 0, 2), bank(2, 0, 2), ("ps", 2, 3))
-    pick("wb", 0, "pb", 0, 128, "wl", 0, 1)
-    quant("wb", 16, 128, "l2t", 0)
+    mm(2, 128, "cbt", 0, "ce", CX)
+    ts(("win", 0, 1), ("rk", 0, 1), 15.5, A.is_lt)
+    fill(("pre", 0, 8), 0.0)
+    ts(("wl", 0, 1), bank(2, 0, 1), bank(2, 1, 2), A.add)
+    copy(("al", nat, nat + 2), bank(2, 0, 2))
+    pick("wb", at + 1 if at else 0, "pb", 0, 128, "wl", 0, 1)
+    quant("wb", 0 if at else K, 128, "al", 0 if at else nat)
 
-    for codes, hs in ((True, far), (False, near)):
-        nm = "wb" if codes else "wbs"
-        before("g", [(nm, 0, SEG)])
-        src, dst = mxv("wb", 0, SEG, codes), mxv("land2", me[0], me[1], codes)
-        g.remote_dma_fused([
-            RemoteDMATransfer(dst_ids=[did(x) for x in hs], dma_engine_mask=bits(hop), remote_sem=T.sem.h2, srcs=[src], dsts=[mxv("hd", 0, SEG, codes)] * 2),
-            RemoteDMATransfer(dst_ids=[did(x) for x in direct], dma_engine_mask=bits(off), remote_sem=T.sem.arr2, srcs=[src], dsts=[dst] * 3),
-        ], local_sem=T.sem.ls)
-        left[0] += len(hop) + len(off)
-    copymx("s", "land2", me[0], "wb", 0, SEG)
+    before("g", [("wb", at, at + SEG), ("wbs", window, window + 4 * SEG)])
+    g.remote_dma_fused([
+        RemoteDMATransfer(dst_ids=[did(x) for x in far], dma_engine_mask=bits(hop), remote_sem=T.sem.h2, srcs=[mxv("wb", at, at + SEG, True)],
+                          dsts=[mxv("hd", 0, SEG, True)] * 2),
+        RemoteDMATransfer(dst_ids=[did(x) for x in near], dma_engine_mask=bits(off), remote_sem=T.sem.h2, srcs=[mxv("wb", window, window + 4 * SEG, False)],
+                          dsts=[mxv("hd", 0, 4 * SEG, False)] * 2),
+    ], local_sem=T.sem.ls2)
+    for codes in (True, False):
+        g.remote_dma_fused([RemoteDMATransfer(dst_ids=[did(x) for x in direct[:2]], dma_engine_mask=bits(off), remote_sem=T.sem.arr2,
+                                              srcs=[mxv("wb", at, at + SEG, codes)], dsts=[mxv("land2", me[0], me[1], codes)] * 2)], local_sem=T.sem.ls2)
+    arrive("ls2", len(hop) + 3 * len(off), [])
 
-    ts(T.s3[:, 0:3], ("s3", 0, 3), T.cum[:, 47:144:48], ("cum", 0, 144), 15.5, None, A.is_lt)
-    ts(T.mk[:, 0:72], ("mk", 0, 72), T.mkrow[:, 0:72], ("mkrow", 0, 72), col(4), None, A.is_equal, None, [("ff", 4, 5)])
-    for c in range(3):
-        ts(T.x2[:, c:96:4], ("x2", 0, 96, 4, c), T.mk[:, 24 * c:24 * c + 24], ("mk", 0, 72), T.s3[:, c:c + 1], None, A.mult, None, [("s3", 0, 3)])
-    ts(T.x2[:, 131:143:4], ("x2", 128, 144), T.m3[:, 0:3], ("m3", 0, 3), T.rk[:, 0:1], 128.0, A.is_gt, A.mult, [("rk", 0, 1)])
-    quant("c2", 0, 128, "x2", 0)
-    mm(3, 128, "ce", CSE, "c2", 0)
     for b in range(4):
         mm(4 + b, 128, "ce", 128 * b, "pb", 0)
-    for e in range(4):
-        act(T.st2[:, e:512:4], ("st2", 0, 512, 4, e), T.ident[:, 3:515:4], ("ident", 0, 516), F.Copy, scale=(8.0, 8.0, 1.0, 0.0)[e])
-    quant("qw", 0, 128, "wt", 0)
-    ts(T.tq2[:, 0:24], ("tq2", 0, 24), bank(3, 0, 24), ("ps", 3, 4), 384.0, col(0), A.mult, A.add, [("ff", 0, 1)])
-    tt(T.te[:, 0:3], ("te", 0, 3), bank(3, 32, 35), ("ps", 3, 4), T.mc[:, 0:3], ("mc", 0, 3), A.add)
-    tt(T.tq[:, 0:24], ("tq", 0, 24), T.tq2[:, 0:24], ("tq2", 0, 24), T.row16k[:, 0:24], ("row16k", 0, 24), A.add)
-    copy(T.off3[:, 0:24], ("off3", 0, 24), T.tq[:, 0:24], ("tq", 0, 24))
-    pick("eo", 0, "qq", Q0, 1024, "off3", 0, 24)
-    dma("s", T.oc[:, 0:1536], T.eo[:, 0:384].bitcast(dt.uint8), [("eo", 0, 384)], [("oc", 0, 1)])
-    for k in range(4):
-        dma("s", T.osc[4 * k:4 * k + 4, 0:384], T.eos[32 * k:32 * k + 4, 0:384], [("eos", 0, 384)], [("osc", k, k + 1)])
-    copy(T.elist[:, 0:3], ("elist", 0, 3), T.te[:, 0:3], ("te", 0, 3))
+    ts(("oht", 1, 512, 4), jr, col(0), A.is_equal, ("win", 0, 1), A.mult)
     for b in range(4):
-        tt(T.lt[:, b:192:4], ("lt", 0, 192, 4, b), T.at[:, b:384:8], ("at", 0, 384), bank(4 + b, 0, 48), ("ps", 4 + b, 5 + b), A.subtract)
-    quant("pb", 128, 128, "lt", 0)
-    pick("eo", 384, "pb", 0, 256, "elist", 0, 3)
-    dma("s", T.oc[:, 1536:1728], T.eo[:, 384:432].bitcast(dt.uint8), [("eo", 384, 432)], [("oc", 1, 2)])
-    for k in range(4):
-        dma("s", T.osc[4 * k:4 * k + 4, 384:432], T.eos[32 * k:32 * k + 4, 384:432], [("eos", 384, 432)], [("osc", 4 + k, 5 + k)])
+        tt(("al", 192 + b, 384, 4), ("so", SW * b + B + 7, SW * b + SW, 8), bank(4 + b, 0, 48), A.subtract)
+    quant("c3", 0, 128, "oht", 0)
+    mm(3, 128, "c3", 0, "ce", CX + WE - WN)
+    quant("pb", 128, 128, "al", 192)
+    tt(("te", 0, 3), bank(3, 0, 3), ("nk", 0, 3), A.add)
+    fill(("nbt", 0, 32), 0.0)
+    copy(("elist", 0, 3), ("te", 0, 3))
     quant("ce", CS2, 128, "st2", 0)
-    fill("nbt", 0, 32, 0.0)
+    pick("eo", P, "pb", 0, 256, "elist", 0, 3)
+    store(P, P + B)
+    w0 = K if at else 0
+    mm(4, 128, "qw", 0, "wb", w0)
+    mm(5, 128, "ce", CS2, "wb", w0)
+    act(("ysb", K * rank, K * rank + K), bank(4, 112, 128) if at else bank(4, 0, K), F.Copy)
+    copy(("pre", rank, rank + 1), bank(5, 111, 112) if at else bank(5, K, K + 1))
+    finish("g", "cdl")
 
     arrive("arr2", 7 * 2 * len(off), [(n, SEG * s, SEG * s + SEG) for s in range(8) if s != rank for n in ("land2", "land2s")])
-    mm(1, 136, "qw", 0, "land2", 0)
-    mm(0, 136, "qw", 0, "land2", 0)
-    mm(3, 136, "ce", CS2, "land2", 0)
-    for q in range(3, 8):
-        act(T.ysb[:, 16 * q:16 * q + 16], ("ysb", 16 * q, 16 * q + 16), bank(1, SEG * q, SEG * q + 16), ("ps", 1, 2), F.Copy)
-    for q in range(3):
-        copy(T.ysb[:, 16 * q:16 * q + 16], ("ysb", 16 * q, 16 * q + 16), bank(0, SEG * q, SEG * q + 16), ("ps", 0, 1))
-    copy(T.nbt[:, 0:8], ("nbt", 0, 8), bank(3, K, 136, SEG), ("ps", 3, 4))
-    op("v", lambda: v.transpose(T.nbx[:, 0:32], T.nbt[:, 0:32]), [("nbt", 0, 32)], [("nbx", 0, 32)])
-    dma("s", T.y[:, 0:48], T.ysb[:, 0:48], [("ysb", 0, 48)], [("y", 0, 48)])
+    mm(1, ZC, "qw", 0, "land2", 0)
+    mm(0, ZC, "qw", 0, "land2", 0)
+    mm(3, ZC, "ce", CS2, "land2", 0)
+    for j in range(4):
+        lo, hi = 0, 2 * K
+        if rank == 2 * j: lo = K
+        if rank == 2 * j + 1: hi = K
+        o, c0 = ("ysb", 2 * K * j + lo, 2 * K * j + hi), 2 * SEG * j + 1
+        if j < 2:
+            act(o, bank(1, c0 + lo, c0 + hi), F.Copy)
+        else:
+            copy(o, bank(0, c0 + lo, c0 + hi))
+    dma("a", T.y[:, 0:128], T.ysb[:, 0:128], [("ysb", 0, 128)], [("y", 0, 128)])
+    for x in range(2):
+        tt(("nbt", x, 8, 2), bank(3, (2 * SEG - 1) * x, ZC, 2 * SEG), ("pre", x, 8, 2), A.add)
+    turn(("nbx", 0, 32), ("nbt", 0, 32))
     dma("s", T.nb[0:1, 0:128], T.nbx[0:8, 0:16], [("nbx", 0, 32)], [("nb", 0, 1)])
-    dma("a", T.y[:, 48:128], T.ysb[:, 48:128], [("ysb", 48, 128)], [("y", 48, 128)])
-    finish({"ls": left[0]})
+    finish("g")

from concourse.bass import DstId, RemoteDMATransfer
from concourse.mybir import dt, AluOpType, AxisListType, ActivationFunctionType

P, B, K = 384, 48, 16
SEG = K + 1
LW = 144
ZC = 8 * SEG
TINY = 2.0 ** -120
H0, L0, Q0, E0 = 16, 144, 256, 640
S0 = 96
PW = 128
CW, SL, CS3, CS2, CX, CALL = 512, 652, 908, 1292, 1420, 1574
WN, WX, WE, WZ, WALL = 24, 26, 50, 54, 178
SW = B + P
X4, U8 = "float8_e4m3fn_x4", "uint8"

SCRATCH = {"ps": ("psum", [128, 4096], "float32")}


def _buf(name, n, d):
    SCRATCH[name] = ("sbuf", [128, n], d)


for _n, _w in (("qe", 384), ("ce", CALL), ("cu", 128), ("qq", 1024), ("sc", 288), ("hc", 192), ("hd", 68), ("land", LW), ("pq", 384), ("fx", 384),
               ("pb", 256), ("cbt", 128), ("wb", 144), ("land2", 136), ("eo", 432), ("c2", 128), ("c3", 128), ("qw", 128)):
    _buf(_n, _w, X4)
    _buf(_n + "s", _w, U8)
for _n, _w in (("et", 1536), ("gt", 1536), ("h", 1536), ("lf", 1536), ("ut", 8), ("ft", 192), ("wt", 512), ("ident", 520), ("pj", 128), ("jr", 128),
               ("zt", 768), ("ur", 512), ("hh", 528), ("ow1", 512), ("slt", 1024), ("fxt", 1536), ("st3", 520), ("sta", 128),
               ("bb", 144), ("d0", 144), ("cum", 144), ("dx", 384), ("st2", 512), ("al", 704), ("oht", 512), ("so", 4 * SW), ("bt", 48)):
    _buf(_n, _w, "bfloat16")
for _n, _w in (("ff", 40), ("own", 48), ("ow2", 48), ("ow3", 48), ("row", 144), ("nk", 24), ("xa", 48), ("xb", 4), ("thr", 144), ("thr2", 48),
               ("zs", 384), ("zg", 96), ("zt2", 64), ("tt", 144), ("t3", 4), ("t4", 4), ("s3", 4), ("tin", 32), ("tto", 32), ("pf", 4), ("pg", 4),
               ("junk", 24), ("sm", 4), ("sa", 4), ("ba", 4), ("zca", 4), ("rk", 4), ("win", 4), ("tq", 48), ("tq2", 24), ("zab", 48), ("te", 4),
               ("ysb", 128), ("pre", 8), ("nbt", 32), ("nbx", 32)):
    _buf(_n, _w, "float32")
for _n, _w in (("pidx", 4), ("ii", 12)):
    _buf(_n, _w, "int32")
for _n, _w in (("goff", 6), ("off1", 12), ("off3", 24), ("off4", 24), ("plist", 4), ("wl", 2), ("elist", 4)):
    _buf(_n, _w, "uint16")

SEMAPHORES = ["cv", "ct", "ca", "cg", "ls1", "ls2", "arr1", "arr2", "h1", "h2"] + ["d%d" % _k for _k in range(40)]


def roles(core, T, topo):
    same = [d for d in T.cores if topo.same_plane(core, d)]
    cross = [d for d in T.cores if d != core and d not in same]
    own = sorted(same + [core])
    x = own.index(core)
    direct = own[x + 1:] + own[:x]
    hs = [c for c in topo.cores_of(core) if c not in T.cores and all([topo.may_write(c, d) for d in cross])]
    near = [c for c in hs if topo.die(c) == topo.die(core)][:2]
    far = [c for c in hs if topo.die(c) != topo.die(core)][:2]
    ranks = [T.rank_of(c) for c in sorted(cross)] + [T.rank_of(c) for c in own]
    units = [(ranks[2 * t], ranks[2 * t + 1]) for t in range(4)]
    return direct, units, near, far


def bits(es):
    m = 0
    for e in es:
        m |= 1 << e
    return m


def split(engines, j, flip):
    q = len(engines) // 4
    cut = [0, q, 2 * q, 4 * q] if flip else [0, 2 * q, 3 * q, 4 * q]
    return engines[cut[j]:cut[j + 1]]


def winners_at(r):
    return (127, 76) if r % 2 == 0 else (0, 0)


def tracker(g, T):
    eng = {"v": g.vector, "t": g.tensor, "a": g.scalar, "g": g, "s": g.sync}
    names = {"v": "cv", "t": "ct", "a": "ca", "g": "cg"}
    cnt, known, waited, hist, nd = {}, {q: {} for q in eng}, {}, {}, [0]

    def clash(a, b):
        if a[0] == "ps":
            return a[1] // 512 == b[1] // 512
        if a[2] <= b[1] or b[2] <= a[1]:
            return False
        if len(a) > 3 and len(b) > 3:
            return not set(range(*a[1:4])).isdisjoint(range(*b[1:4]))
        return True

    def wait(q, toks):
        toks = [t for t in toks if known[q].get(t[0], 0) < t[1]]
        best = {}
        for t in toks:
            if t[0] not in best or best[t[0]][1] < t[1]:
                best[t[0]] = t
        for t in list(best.values()):
            if any([u is not t and u[2].get(t[0], 0) >= t[1] for u in best.values()]):
                continue
            eng[q].wait_ge(T.sem[t[0]], t[1])
            waited[t[0]] = max(waited.get(t[0], 0), t[1])
            for s, c in t[2].items():
                known[q][s] = max(known[q].get(s, 0), c)

    def hazards(q, reads, writes):
        toks = []
        for rs, any_ in ((reads, False), (writes, True)):
            for r in rs:
                for (x, w, tok, e) in hist.get(r[0], []):
                    if (e != q if r[0] == "ps" else w or any_) and clash(r, x): toks.append(tok)
        return toks

    def note(q, reads, writes, tok):
        for r in reads: hist.setdefault(r[0], []).append((r, False, tok, q))
        for r in writes: hist.setdefault(r[0], []).append((r, True, tok, q))

    def op(q, fn, reads, writes):
        wait(q, hazards(q, reads, writes))
        s = names[q]
        cnt[s] = cnt.get(s, 0) + 1
        fn().then_inc(T.sem[s], 1)
        note(q, reads, writes, (s, cnt[s], dict(known[q], **{s: cnt[s]})))

    def dma(q, out, in_, reads, writes):
        wait(q, hazards("dma", reads, writes))
        s = "d%d" % nd[0]
        nd[0] += 1
        eng[q].dma_start(out, in_).then_inc(T.sem[s], 16)
        cnt[s] = 16
        note("dma", reads, writes, (s, 16, dict(known[q], **{s: 16})))

    def before(q, reads):
        wait(q, hazards("dma", reads, []))

    def arrive(s, total, writes):
        cnt[s] = total
        note("far", [], writes, (s, total, {s: total}))

    def finish(q, only=None):
        for s in cnt:
            if waited.get(s, 0) < cnt[s] and (only is None or s[0] in only):
                eng[q].wait_ge(T.sem[s], cnt[s])
                waited[s] = cnt[s]

    return op, dma, before, arrive, finish


def helper(g, core, T, topo):
    home = [c for c in T.cores if core in topo.cores_of(c)]
    if not home:
        return
    src = home[0]
    s = T.rank_of(src)
    direct, units, near, far = roles(src, T, topo)
    if core in far:
        t, codes = far.index(core), True
    elif core in near:
        t, codes = near.index(core), False
    else:
        return
    a, b = [T.cores[r] for r in units[t]]

    def did(d):
        rid, pid = topo.addr(d, core)
        return DstId(rid=rid, pnc=pid)

    def view(n, lo):
        return T[n][:, lo:lo + SEG].bitcast(dt.uint8) if codes else T[n + "s"][:, lo:lo + SEG]
    es = topo.engines(core, a)
    half = len(es) // 2
    o = 0 if codes else S0 + B * t
    g.wait_ge(T.sem.h1, half)
    g.remote_dma_fused([
        RemoteDMATransfer(dst_ids=[did(a)], dma_engine_mask=bits(es[:half]), remote_sem=T.sem.arr1, srcs=[view("hc", o)], dsts=[view("land", SEG * s)]),
        RemoteDMATransfer(dst_ids=[did(b)], dma_engine_mask=bits(es[half:]), remote_sem=T.sem.arr1, srcs=[view("hc", o + B - SEG)], dsts=[view("land", SEG * s)]),
    ], local_sem=T.sem.ls1)
    to = [a, b] + (direct[2:] if t == 0 else [])
    at, window = winners_at(s)
    g.wait_ge(T.sem.ls1, len(es))
    g.wait_ge(T.sem.h2, len(es))
    g.remote_dma_fused([RemoteDMATransfer(dst_ids=[did(x) for x in to], dma_engine_mask=bits(es), remote_sem=T.sem.arr2, srcs=[view("hd", 0 if codes else at - window)],
                                          dsts=[view("land2", SEG * s)] * len(to))], local_sem=T.sem.ls2)
    g.wait_ge(T.sem.ls2, len(es))


def rank_program(g, core, T, topo):
    rank = T.rank_of(core)
    if rank is None:
        return helper(g, core, T, topo)
    direct, units, near, far = roles(core, T, topo)
    op, dma, before, arrive, finish = tracker(g, T)
    A, F = AluOpType, ActivationFunctionType
    v, ten, sca = g.vector, g.tensor, g.scalar

    def ap(x):
        if not isinstance(x, tuple):
            return x
        return T[x[0]][:, x[1]:x[2]:x[3]] if len(x) > 3 else T[x[0]][:, x[1]:x[2]]

    def held(*xs):
        return [x for x in xs if isinstance(x, tuple)]

    def bank(k, lo, hi, step=1):
        return ("ps", 512 * k + lo, 512 * k + hi, step)

    def col(k):
        return ("ff", k, k + 1)

    def fill(o, val):
        op("v", lambda: v.memset(ap(o), val), [], [o])

    def iota(o, pattern, base=0, cm=0):
        op("g", lambda: g.iota(ap(o), pattern, base, cm, allow_small_or_imprecise_dtypes=True), [], [o])

    def ts(o, i, s1, op0, s2=None, op1=None):
        if op1 is None:
            op("v", lambda: v.tensor_scalar(ap(o), ap(i), ap(s1), None, op0), held(i, s1), [o])
        else:
            op("v", lambda: v.tensor_scalar(ap(o), ap(i), ap(s1), ap(s2), op0, op1), held(i, s1, s2), [o])

    def tt(o, i0, i1, opx):
        op("v", lambda: v.tensor_tensor(ap(o), ap(i0), ap(i1), opx), [i0, i1], [o])

    def copy(o, i):
        op("v", lambda: v.tensor_copy(ap(o), ap(i)), [i], [o])

    def act(o, i, func, bias=None, scale=None, total=None):
        kw = {}
        if bias is not None: kw["bias"] = ap(bias)
        if scale is not None: kw["scale"] = ap(scale)
        if total is not None: kw["accum_out"] = ap(total)
        op("a", lambda: sca.activation(ap(o), ap(i), func, **kw), held(i, bias, scale), held(o, total))

    def const(o, val=0.0):
        n = len(range(*o[1:]))
        if isinstance(val, float) and val == 0.0:
            act(o, ("ident", 0, n), F.Copy, scale=0.0)
        else:
            act(o, ("ident", 0, n), F.Identity, bias=val, scale=0.0)

    def gather(q, o, w, l):
        if q == "v":
            op("v", lambda: v.tensor_copy(ap(o), ap(w).indirect(ap(l))), [w, l], [o])
        else:
            op("a", lambda: sca.activation(ap(o), ap(w).indirect(ap(l)), F.Copy), [w, l], [o])

    def scan(o, d, i):
        op("v", lambda: v.tensor_tensor_scan(ap(o), ap(d), ap(i), 0.0, A.mult, A.add), [d, i], [o])

    def turn(o, i):
        op("v", lambda: v.transpose(ap(o), ap(i)), [i], [o])

    def reduce(o, i, opx, **kw):
        op("v", lambda: v.tensor_reduce(ap(o), ap(i), AxisListType.X, opx, **kw), [i], [o])

    def quant(n, c, w, tile, a):
        op("v", lambda: v.quantize_mx(T[n][:, c:c + w], T[n + "s"][:, c:c + w], T[tile][:, a:a + 4 * w]),
           [(tile, a, a + 4 * w)], [(n, c, c + w), (n + "s", c, c + w)])

    def mm(k, w, ln, l0, rn, r0, start=True, stop=True):
        op("t", lambda: ten.matmul_mx(T.ps[:, 512 * k:512 * k + w], T[ln][:, l0:l0 + 128], T[ln + "s"][:, l0:l0 + 128],
                                      T[rn][:, r0:r0 + w], T[rn + "s"][:, r0:r0 + w], start, stop),
           [(ln, l0, l0 + 128), (ln + "s", l0, l0 + 128), (rn, r0, r0 + w), (rn + "s", r0, r0 + w)], [bank(k, 0, w)])

    def pick(on, o0, sn, w0, w1, ln, e0, e1):
        w = 16 * (e1 - e0)
        op("v", lambda: v.tensor_copy(T[on][:, o0:o0 + w].bitcast(dt.uint32), T[sn][:, w0:w1].bitcast(dt.uint32).indirect(T[ln][:, e0:e1])),
           [(sn, w0, w1), (ln, e0, e1)], [(on, o0, o0 + w)])
        op("a", lambda: sca.activation(T[on + "s"][:, o0:o0 + w], T[sn + "s"][:, w0:w1].indirect(T[ln][:, e0:e1]), F.Copy),
           [(sn + "s", w0, w1), (ln, e0, e1)], [(on + "s", o0, o0 + w)])

    def copyplane(q, dn, d0, sn, s0, w):
        dma(q, T[dn + "s"][:, d0:d0 + w], T[sn + "s"][:, s0:s0 + w], [(sn + "s", s0, s0 + w)], [(dn + "s", d0, d0 + w)])

    def copymx(q, dn, d0, sn, s0, w):
        dma(q, T[dn][:, d0:d0 + w].bitcast(dt.uint8), T[sn][:, s0:s0 + w].bitcast(dt.uint8), [(sn, s0, s0 + w)], [(dn, d0, d0 + w)])
        copyplane(q, dn, d0, sn, s0, w)

    def store(lo, hi):
        dma("s", T.oc[:, 4 * lo:4 * hi], T.eo[:, lo:hi].bitcast(dt.uint8), [("eo", lo, hi)], [("oc", lo, hi)])
        for k in range(4):
            dma("s", T.osc[4 * k:4 * k + 4, lo:hi], T.eos[32 * k:32 * k + 4, lo:hi], [("eos", lo, hi)], [("osc%d" % k, lo, hi)])

    def load(q, dst, src, k):
        sl = slice(4 * PW * k, 4 * PW * k + 4 * PW)
        dma(q, T[dst][:, sl], T[src][:, sl], [], [(dst, 4 * PW * k, 4 * PW * k + 4 * PW)])
    load("s", "et", "er", 0)
    dma("a", T.ut[:, 0:4], T.u[:, 0:4], [], [("ut", 0, 8)])
    load("a", "gt", "gr", 0)
    load("s", "et", "er", 1)
    load("a", "gt", "gr", 1)
    load("s", "et", "er", 2)
    load("a", "gt", "gr", 2)

    op("g", lambda: g.iota(T.pidx[:, 0:1], [[0, 1]], 0, 1), [], [("pidx", 0, 4)])
    iota(("pj", 0, 128), [[1, 128]], 0, -1)
    iota(("row", 0, 144), [[-16, 3], [1, 48]])
    iota(("jr", 0, 128), [[0, 8], [1, 16]])
    jr = ("jr", 0, 128)

    def ibit(k, s1, op0, s2=None, op1=None):
        ts(("ii", k, k + 1), ("pidx", 0, 1), s1, op0, s2, op1)
    fill(("ident", 0, 520), 0.0)
    ibit(0, 15, A.bitwise_and)
    ibit(1, 4, A.logical_shift_right)
    ibit(2, 4, A.logical_shift_right, 14, A.bitwise_and)
    ibit(3, 2, A.logical_shift_right, 3, A.bitwise_and)
    copy(("ff", 0, 4), ("ii", 0, 4))
    ts(("ident", 3, 515, 4), ("pj", 0, 128), 0.0, A.is_equal)
    ts(col(9), col(1), float(rank), A.is_equal)

    const(("ow1", 0, 512), col(9))
    for h in range(2):
        op("g", lambda: g.affine_select(T.slt[:, 512 * h:512 * h + 512], T.ow1[:, 0:512], [[0, 4], [-2, 32], [16, 4]], A.is_equal, 0.0, -16 * rank - h, 1),
           [("ow1", 0, 512)], [("slt", 512 * h, 512 * h + 512)])
    iota(("st3", 0, 520), [[0, 520]])
    const(("own", 0, 48), 99.0)
    act(col(16), col(0), F.Identity, col(1), 8.0)
    for t in range(4):
        for k, o in ((3 * t, units[t][0]), (3 * t + 2, units[t][1])):
            const(("own", 4 * k, 4 * k + 4), float(o))
    act(col(27), col(3), F.Identity, 128.0, 32.0)
    act(("ow2", 0, 48), ("own", 0, 48), F.Abs, col(1), -1.0)
    act(col(21), col(16), F.Identity, 112.0)
    act(("ff", 22, 25), ("row", 0, 3), F.Identity, col(27), 128.0)
    act(("ow3", 0, 48), ("ow2", 0, 48), F.Relu, 1.0, -1.0)
    act(col(20), col(27), F.Identity, col(21), -1.0)
    for e in range(4):
        act(("ur", e, 512, 4), ("pj", 0, 128), F.Identity, ("ut", e, e + 1), 0.0)
    const(("zt", 0, 512))
    act(col(17), col(0), F.Identity, col(2), 8.0)
    act(col(10), col(2), F.Identity, col(1), -1.0)
    for c in range(3):
        act(("zt", c, 48, 4), ("ow3", c, 48, 4), F.Copy, scale=col(22 + c))
    act(("zt", 48, 96), ("ow3", 0, 48), F.Copy, scale=col(20))
    act(col(12), col(10), F.Identity, col(17), 128.0)
    const(("zt", 512, 768))

    BE = ((0, 1, 2, 3), (4, 5, 6, 7), (0, 1, 2, 4))
    BS = (3, 5, 6)

    def errors(k):
        quant("qe", PW * k, PW, "et", 4 * PW * k)
        for b in range(4):
            mm(BE[k][b], PW, "ce", 128 * b, "qe", PW * k)

    def values(k, b):
        lo, hi = 4 * PW * k + b, 4 * PW * k + 4 * PW
        tt(("h", lo, hi, 4), bank(BE[k][b], 0, PW), ("gt", lo, hi, 4), A.add)

    def codes_of(k):
        quant("qq", Q0 + PW * k, PW, "h", 4 * PW * k)

    def scores(k):
        mm(BS[k], PW, "cu", 0, "qq", Q0 + PW * k)
        act(("zs", PW * k, PW * k + PW), bank(BS[k], 0, PW), F.Abs)
    for b in range(4):
        quant("ce", 128 * b, 128, "ident", 3 - b)
    errors(0)
    ibit(4, 1, A.bitwise_and)
    ibit(5, 15, A.bitwise_and, 1, A.logical_shift_right)
    ibit(6, 7, A.bitwise_and)
    values(0, 0)
    values(0, 1)
    errors(1)
    values(0, 2)
    values(0, 3)
    values(1, 0)
    codes_of(0)
    values(1, 1)
    errors(2)
    values(1, 2)
    values(1, 3)
    quant("cu", 0, 128, "ur", 0)
    codes_of(1)
    scores(0)
    scores(1)
    act(col(28), col(0), F.Copy, scale=TINY)
    const(("d0", 0, 144), 1.0)
    act(("thr", 0, 144), ("row", 0, 144), F.Relu, col(28), -TINY)
    const(("d0", 0, 144, 48))
    for b in range(4):
        values(2, b)
    ts(("goff", 0, 3), ("row", 0, 3), 128.0, A.mult, col(16), A.add)
    codes_of(2)
    scores(2)
    for b in range(2):
        mm(b, 384, "ce", 128 * b, "qq", Q0)
    before("s", [("gt", 1024, 1536)])
    dma("s", T.ft[:, 0:192], T.fo[:, 0:192], [], [("ft", 0, 192)])
    copyplane("s", "sc", 0, "ce", 0, S0)
    dma("s", T.wt[:, 0:512], T.w[:, 0:512], [], [("wt", 0, 512)])
    ts(("goff", 3, 4), col(17), 257.0, A.add)
    ts(("goff", 4, 6), ("row", 0, 2), col(12), A.add)
    quant("ce", CW, 140, "zt", 0)
    quant("land2", 0, ZC, "zt", 4 * WZ)
    copymx("s", "land", ZC, "ce", CW + WZ, 2)
    second = [u for u in units if rank in u][0][1] == rank
    lp, dlt = (0, 1) if second else (K, 0)

    gather("v", ("zg", 0, 96), ("zs", 0, 384), ("goff", 0, 6))
    const(("hh", 512, 528))
    const(("hh", 3, 512, 4))
    copy(("ff", 4, 7), ("ii", 4, 7))
    turn(("zt2", 0, 64), ("zg", 32, 96))
    ts(col(26), col(1), 2.5, A.is_lt)
    for c, x in ((0, 32), (1, 48)):
        ts(("tt", 48 * c, 48 * c + 48), ("zg", 0, 48), ("zt2", x, x + 1), A.subtract, -1.0, A.mult)
    act(("tt", 96, 144), ("zg", 0, 48), F.Identity, ("zt2", 0, 1), -1.0)
    const(("fxt", 0, 384))
    tt(("bb", 0, 144), ("tt", 0, 144), ("thr", 0, 144), A.is_lt)
    scan(("cum", 0, 144), ("d0", 0, 144), ("bb", 0, 144))
    ranks = ("cum", 47, 144, 48)
    act(("t4", 0, 3), ranks, F.Identity, -3600.0, 240.0)
    for c in range(3):
        ts(("hh", c, 512, 4), jr, ("cum", 48 * c + 47, 48 * c + 48), A.is_equal)
    tt(("hh", 512, 515), ("t4", 0, 3), ranks, A.max)
    quant("qq", H0, 132, "hh", 0)
    for k in range(2):
        mm(2, 128, "qq", H0, "ce", CW + 12 * k, k == 0, k == 1)
    mm(7, 384, "ce", 256, "qq", Q0)
    mm(3, 384, "ce", 384, "qq", Q0)
    quant("ce", SL, 256, "slt", 0)
    ts(("off1", 0, 12), bank(2, 0, 12), float(L0 - 128), A.add)
    const(("fxt", 384, 896))
    act(("t3", 0, 3), ranks, F.Sign, -15.5)
    pick("sc", S0, "qq", 128, 640, "off1", 0, 6)
    pick("sc", S0 + 96, "qq", 128, 640, "off1", 6, 12)

    def did(d):
        rid, pid = topo.addr(d, core)
        return DstId(rid=rid, pnc=pid)

    def mxv(n, lo, hi, codes):
        return T[n][:, lo:hi].bitcast(dt.uint8) if codes else T[n + "s"][:, lo:hi]
    off = topo.engines(core, direct[0])
    hop = [e for e in topo.engines(core, far[0]) if e not in off]
    half = len(hop) // 2
    run = {}
    for t in range(4):
        run[units[t][0]] = S0 + B * t
        run[units[t][1]] = S0 + B * t + B - SEG
    me = (SEG * rank, SEG * rank + SEG)
    before("g", [("sc", S0, S0 + 96), ("scs", 0, S0 + 96), ("land2", 0, ZC), ("land2s", 0, ZC)])
    g.remote_dma_fused(
        [RemoteDMATransfer(dst_ids=[did(far[t])], dma_engine_mask=bits(hop[half * t:half * t + half]), remote_sem=T.sem.h1,
                           srcs=[mxv("sc", S0 + B * t, S0 + B * t + B, True)], dsts=[mxv("hc", 0, B, True)]) for t in range(2)] +
        [RemoteDMATransfer(dst_ids=[did(near[t])], dma_engine_mask=bits(off[half * t:half * t + half]), remote_sem=T.sem.h1,
                           srcs=[mxv("sc", 0, 4 * B, False)], dsts=[mxv("hc", 0, 4 * B, False)]) for t in range(2)], local_sem=T.sem.ls1)
    for codes in (True, False):
        before("g", [("sc" if codes else "scs", S0 + 96, S0 + 192)])
        g.remote_dma_fused([RemoteDMATransfer(dst_ids=[did(direct[j])], dma_engine_mask=bits(split(off, j, not codes)), remote_sem=T.sem.arr1,
                                              srcs=[mxv("sc", run[T.rank_of(direct[j])], run[T.rank_of(direct[j])] + SEG, codes)],
                                              dsts=[mxv("land", me[0], me[1], codes)]) for j in range(3)], local_sem=T.sem.ls1)
    arrive("ls1", len(hop) + 3 * len(off), [("gone1", 0, 1)])
    copymx("s", "land", me[0], "sc", run[rank], SEG)
    iota(("al", 192, 704), [[0, 512]])
    iota(("oht", 0, 512), [[0, 512]])

    def left_over(b, n):
        tt(("lf", b, 1536, 4), ("h", b, 1536, 4), bank(n, 0, 384), A.subtract)
    const(("fxt", 896, 1408))
    const(("fxt", 1408, 1536))
    act(("s3", 0, 3), ("t3", 0, 3), F.Identity, 0.5, -0.5)
    act(col(19), col(4), F.Identity, col(1), 8.0)
    for e in range(4):
        act(("fxt", e, 1536, 32), ("ft", e, 192, 4), F.Copy)
    act(("xa", 0, 48), ("row", 48, 96), F.Abs, col(5), -1.0)
    act(("xb", 0, 3), ("row", 0, 3), F.Abs, col(1), -1.0)
    act(col(25), col(26), F.Copy, scale=16.0)
    for c in range(3):
        act(("zt", 4 * WX + c, 4 * WE, 4), ("xa", 16 - 8 * c, 40 - 8 * c), F.Relu, float(P), -float(P))
    act(("zt", 4 * WE + 1, 4 * WE + 13, 4), ("xb", 0, 3), F.Relu, 128.0, -128.0)
    act(("zt", 4 * WN, 4 * WN + 1), col(1), F.Copy, scale=col(25))
    act(("zt", 4 * WN + 4, 4 * WN + 5), col(0), F.Copy, scale=col(26))
    act(("sta", 0, 128), jr, F.Abs, col(0), -1.0)
    act(("nk", 0, 24), ("row", 0, 24), F.Identity, col(0), 16.0)
    act(("st3", 3, 515, 4), ("sta", 0, 128), F.Relu, col(9), -1.0)
    left_over(2, 7)
    left_over(3, 3)
    left_over(0, 0)
    quant("fx", 0, 384, "fxt", 0)
    BD = (4, 5, 6)
    for b in range(3):
        mm(BD[b], 384, "ce", 128 * b, "fx", 0, True, False)
    mm(7, 256, "ce", 384, "fx", 0, True, False)
    mm(3, 128, "ce", 384, "fx", 256, True, False)
    for c in range(3):
        ts(("hh", c, 512, 4), jr, col(19), A.is_equal, ("s3", c, c + 1), A.mult)
    ts(col(18), col(6), float(SEG), A.mult, float(dlt), A.add)
    quant("c2", 0, 128, "hh", 0)
    quant("ce", CX, WALL - WN, "zt", 4 * WN)
    mm(2, 128, "c2", 0, "ce", CX + WX - WN)
    left_over(1, 1)
    tt(("tq2", 0, 24), bank(2, 0, 24), ("nk", 0, 24), A.add)
    quant("qq", E0, 384, "lf", 0)
    copy(("off3", 0, 24), ("tq2", 0, 24))
    for c in range(3):
        quant("ce", CS3 + 128 * c, 128, "st3", 3 - c)
    const(("dx", 0, 384), 1.0)
    for e in range(4):
        act(("so", SW * e, SW * e + B), ("ft", e, 192, 4), F.Copy)
    const(("dx", 0, 384, 8))
    act(col(29), ("pj", 0, 1), F.Copy, scale=-TINY)
    act(("sa", 0, 3), ("nk", 0, 3), F.Identity, -27.5, -3.5)
    act(("ba", 0, 3), ("nk", 0, 3), F.Identity, 27.5, 4.5)
    act(("thr2", 0, 48), ("row", 0, 48), F.Relu, col(29), -TINY)
    pick("eo", 0, "qq", Q0, 1024, "off3", 0, 24)
    before("s", [("gone1", 0, 1)])
    store(0, P)

    total = 0
    for s in range(8):
        if s == rank: continue
        src = T.cores[s]
        sd = roles(src, T, topo)[0]
        if core in sd:
            es = topo.engines(src, core)
            j = sd.index(core)
            total += len(split(es, j, False)) + len(split(es, j, True))
        else:
            total += len(off)
    arrive("arr1", total, [(n, SEG * s, SEG * s + SEG) for s in range(8) if s != rank for n in ("land", "lands")])
    for h in range(2):
        mm(h, ZC, "ce", SL + 128 * h, "land", 0)
    for k in range(2):
        act(("tin", 16 * k, 16 * k + 8), bank(0, lp, ZC, SEG), F.Copy)
        copy(("tin", 16 * k + 8, 16 * k + 16), bank(1, lp, ZC, SEG))
    for c in range(3):
        mm((2, 0, 1)[c], ZC, "ce", CS3 + 128 * c, "land", 0)
        act(("junk", 8 * c, 8 * c + 8), bank((2, 0, 1)[c], lp, ZC, SEG), F.Sign, -100.0, total=("sm", c, c + 1))
    turn(("tto", 0, 32), ("tin", 0, 32))
    ts(("off4", 0, 24), ("tto", 0, 24), col(18), A.add, float(ZC), A.min)
    pick("pq", 0, "land", 0, LW, "off4", 0, 16)
    pick("pq", 256, "land", 0, LW, "off4", 16, 24)
    mm(7, 256, "ce", 384, "pq", 0, False, True)
    for b in range(3):
        mm(BD[b], 384, "ce", 128 * b, "pq", 0, False, True)
    mm(3, 128, "ce", 384, "pq", 256, False, True)
    act(("pf", 0, 3), ("sm", 0, 3), F.Sign, -7.0)
    at, window = winners_at(rank)
    nat = 508 if at else 192
    const(("al", nat + 2, nat + 3), float(rank))
    for c in range(3):
        act(("pg", c, c + 1), ("pf", c, c + 1), F.Identity, ("ba", c, c + 1), ("sa", c, c + 1))

    def sums(b, lo, hi, n):
        scan(("so", SW * b + B + lo, SW * b + B + hi), ("dx", 0, hi - lo), bank(n, 0, hi - lo))

    def summed(e, b, lo, hi):
        gather(e, ("al", 64 * lo + b, 64 * hi, 4), ("so", SW * b, SW * b + B + 128 * hi), ("plist", lo, hi))
    sums(3, 0, 256, 7)
    sums(0, 0, 384, 4)
    copy(("plist", 0, 3), ("pg", 0, 3))
    summed("a", 3, 0, 2)
    summed("a", 0, 0, 3)
    sums(1, 0, 384, 5)
    summed("a", 1, 0, 3)
    sums(2, 0, 384, 6)
    summed("a", 2, 0, 3)
    sums(3, 256, 384, 3)
    summed("v", 3, 2, 3)
    quant("pb", 0, 128, "al", 0)

    mm(1, 128, "cu", 0, "pb", 0)
    mm(0, 128, "pb", 0, "cu", 0)
    act(("zab", 0, 48), bank(1, 0, 48), F.Abs)
    for e in range(4):
        act(("st2", e, 512, 4), ("ident", 3, 515, 4), F.Copy, scale=(8.0, 8.0, 1.0, 0.0)[e])
    quant("qw", 0, 128, "wt", 0)
    reduce(("zca", 0, 1), bank(0, 0, 1), A.max, apply_absolute_value=True)
    ts(("tq", 0, 48), ("zab", 0, 48), ("zca", 0, 1), A.subtract, -1.0, A.mult)
    tt(("bt", 0, 48), ("tq", 0, 48), ("thr2", 0, 48), A.is_lt)
    reduce(("rk", 0, 1), ("bt", 0, 48), A.add)
    ts(("oht", 0, 512, 4), jr, ("rk", 0, 1), A.is_equal)
    quant("cbt", 0, 128, "oht", 0)
    mm(2, 128, "cbt", 0, "ce", CX)
    ts(("win", 0, 1), ("rk", 0, 1), 15.5, A.is_lt)
    fill(("pre", 0, 8), 0.0)
    ts(("wl", 0, 1), bank(2, 0, 1), bank(2, 1, 2), A.add)
    copy(("al", nat, nat + 2), bank(2, 0, 2))
    pick("wb", at + 1 if at else 0, "pb", 0, 128, "wl", 0, 1)
    quant("wb", 0 if at else K, 128, "al", 0 if at else nat)

    before("g", [("wb", at, at + SEG), ("wbs", window, window + 4 * SEG)])
    g.remote_dma_fused([
        RemoteDMATransfer(dst_ids=[did(x) for x in far], dma_engine_mask=bits(hop), remote_sem=T.sem.h2, srcs=[mxv("wb", at, at + SEG, True)],
                          dsts=[mxv("hd", 0, SEG, True)] * 2),
        RemoteDMATransfer(dst_ids=[did(x) for x in near], dma_engine_mask=bits(off), remote_sem=T.sem.h2, srcs=[mxv("wb", window, window + 4 * SEG, False)],
                          dsts=[mxv("hd", 0, 4 * SEG, False)] * 2),
    ], local_sem=T.sem.ls2)
    for codes in (True, False):
        g.remote_dma_fused([RemoteDMATransfer(dst_ids=[did(x) for x in direct[:2]], dma_engine_mask=bits(off), remote_sem=T.sem.arr2,
                                              srcs=[mxv("wb", at, at + SEG, codes)], dsts=[mxv("land2", me[0], me[1], codes)] * 2)], local_sem=T.sem.ls2)
    arrive("ls2", len(hop) + 3 * len(off), [])

    for b in range(4):
        mm(4 + b, 128, "ce", 128 * b, "pb", 0)
    ts(("oht", 1, 512, 4), jr, col(0), A.is_equal, ("win", 0, 1), A.mult)
    for b in range(4):
        tt(("al", 192 + b, 384, 4), ("so", SW * b + B + 7, SW * b + SW, 8), bank(4 + b, 0, 48), A.subtract)
    quant("c3", 0, 128, "oht", 0)
    mm(3, 128, "c3", 0, "ce", CX + WE - WN)
    quant("pb", 128, 128, "al", 192)
    tt(("te", 0, 3), bank(3, 0, 3), ("nk", 0, 3), A.add)
    fill(("nbt", 0, 32), 0.0)
    copy(("elist", 0, 3), ("te", 0, 3))
    quant("ce", CS2, 128, "st2", 0)
    pick("eo", P, "pb", 0, 256, "elist", 0, 3)
    store(P, P + B)
    w0 = K if at else 0
    mm(4, 128, "qw", 0, "wb", w0)
    mm(5, 128, "ce", CS2, "wb", w0)
    act(("ysb", K * rank, K * rank + K), bank(4, 112, 128) if at else bank(4, 0, K), F.Copy)
    copy(("pre", rank, rank + 1), bank(5, 111, 112) if at else bank(5, K, K + 1))
    finish("g", "cdl")

    arrive("arr2", 7 * 2 * len(off), [(n, SEG * s, SEG * s + SEG) for s in range(8) if s != rank for n in ("land2", "land2s")])
    mm(1, ZC, "qw", 0, "land2", 0)
    mm(0, ZC, "qw", 0, "land2", 0)
    mm(3, ZC, "ce", CS2, "land2", 0)
    for j in range(4):
        lo, hi = 0, 2 * K
        if rank == 2 * j: lo = K
        if rank == 2 * j + 1: hi = K
        o, c0 = ("ysb", 2 * K * j + lo, 2 * K * j + hi), 2 * SEG * j + 1
        if j < 2:
            act(o, bank(1, c0 + lo, c0 + hi), F.Copy)
        else:
            copy(o, bank(0, c0 + lo, c0 + hi))
    dma("a", T.y[:, 0:128], T.ysb[:, 0:128], [("ysb", 0, 128)], [("y", 0, 128)])
    for x in range(2):
        tt(("nbt", x, 8, 2), bank(3, (2 * SEG - 1) * x, ZC, 2 * SEG), ("pre", x, 8, 2), A.add)
    turn(("nbx", 0, 32), ("nbt", 0, 32))
    dma("s", T.nb[0:1, 0:128], T.nbx[0:8, 0:16], [("nbx", 0, 32)], [("nb", 0, 1)])
    finish("g")
